import numpy as np, ml_dtypes
CORES = [78,86,94,102,110,118]
N = 6
BF = ml_dtypes.bfloat16
W, R, P, STEPS, HOPS, SHIFT = 1024, 8192, 512, 3, 3, 2
def parts(rng):
    h = rng.integers(0, 256, (N, 8, 16, P)); w = rng.integers(0, 256, (N, 8, 16, 1)); t = rng.integers(700, 1300, (N, 8, 16, 1))
    m = rng.random((N, 8, W)) < rng.choice(np.array([0.1, 0.25, 0.5]), (N, 8, 1))
    return h, w, t, m, rng.integers(0, R, (N, 8, 16, W)), rng.integers(0, 256, (N, 8, 16, R))
def pack(h, w, t, m, o, r):
    m = m.astype(np.int32); m[..., 0] = 1
    b = lambda v, n: np.ascontiguousarray(v.reshape(N, 128, n)).astype(np.float32).astype(BF)
    i = lambda v, n: np.ascontiguousarray(v.reshape(N, 128, n)).astype(np.int32)
    return {"h0": b(h, P), "w": b(w, 1), "th": i(t, 1), "marks": m, "owner": i(o, W), "hdr": b(r, R)}
def far(rng, h, t, o, r, g, u=None):
    r[:, g] = rng.integers(128, 192, (N, 16, R))
    goal = np.where(np.arange(R) % 2 == 0, 4, 0) + rng.integers(0, 4, (N, R))
    r[:, g, 15] = 128 + ((goal - np.sum(r[:, g, :15], axis=1)) & 63)
    o[:, g] = (o[:, g] & -2) + (np.arange(16) & 1)[:, None]
    h[:, g] = rng.integers(0, 16, (N, 16, P))
    if u is not None: h[:, g, 0] = u >> 4; h[:, g, 1] = u & 15
    h[:, g, 15] = (-np.sum(h[:, g, :15], axis=1)) & 63
    t[:, g] = rng.integers(1300, 1751, (N, 16, 1))
def setup_inputs(rng):
    return pack(*parts(rng))
def setup_inputs_crowd(rng):
    h, w, t, m, o, r = parts(rng)
    w[:, 0::4] = 0; t[:, 0::4] = rng.integers(500, 1100, (N, 2, 16, 1))
    w[:, 1::4] = 0; w[:, 1::4, 0] = rng.integers(1, 4, (N, 2, 1)); h[:, 1::4, 0] = rng.integers(0, 3, (N, 2, P))
    w[:, 2::4] = 128 * rng.integers(0, 2, (N, 2, 16, 1))
    n = P // 16; lane = np.arange(P)
    far(rng, h, t, o, r, 4)
    start = rng.integers(0, n, (N, 16)); start[:, 0::4] = 0; start[:, 1::4] = n - 1; start[:, 3::4] = 1
    near = (lane >> 4) < start[:, lane & 15]
    h[:, 4] = np.where(near[:, None, :], rng.integers(128, 192, (N, 16, P)), h[:, 4])
    k = np.arange(256); found = np.unique((((k * k) >> 5) + k) & (W - 16), return_index=True)[1]
    order = np.argsort(rng.random((N, 16, len(found))), axis=-1)[..., :n]
    far(rng, h, t, o, r, 7, found[order].transpose(0, 2, 1).reshape(N, P))
    w[:, 7] = 0; w[:, 7, 0] = 16; w[:, 7, 1] = 1; m[:, 7] = True
    return pack(h, w, t, m, o, r)
def setup_inputs_ends(rng):
    h, w, t, m, o, r = parts(rng)
    k = np.arange(4096); tops = np.flatnonzero(((((k * k) >> 5) + k) & (W - 16)) == W - 16)
    u = rng.integers(0, 4096, (N, 6, P)); u[..., 0::32] = 0; u[..., 15::32] = rng.choice(tops, u[..., 15::32].shape)
    u[:, 4, 5::8] = rng.choice(tops, u[:, 4, 5::8].shape)
    w[:, :6] = 0; w[:, :6, 0] = 16; w[:, :6, 1] = 1; h[:, :6, 0] = u >> 4; h[:, :6, 1] = u & 15
    m[:, 0] = False; m[:, 1] = True; m[:, 2] = False; m[:, 2, W - 1] = True; m[:, 3] = True; m[:, 3, W - 1] = False; m[:, 4] = False; m[:, 4, 1] = True; m[:, 4, W - 16] = True
    t[:, 0:4:2] = rng.integers(0, 900, (N, 2, 16, 1)); t[:, 1] = rng.choice(np.array([0, 4096]), (N, 16, 1)); t[:, 5] = 0; t[:, 6] = 4096
    w[:, 7] = 255 - rng.integers(0, 16, (N, 16, 1)); h[:, 7] = 255 - rng.integers(0, 24, (N, 16, P)); w[0, 7] = 255; h[0, 7, :, 0::32] = 255
    return pack(h, w, t, m, o, r)
def setup_inputs_ties(rng):
    h, w, t, m, o, r = parts(rng)
    unit = rng.choice(np.array([8, 16]), (N, 8, 1, 1)); h = unit * (h // unit); r = unit * (r // unit)
    t = unit * (t // unit) + rng.choice(np.array([0, 0, 0, 1, -1]), t.shape)
    w[:, :2] = 0; m[:, :2, :16] = True; h[:, 1, :, :16] = 0; h[:, 1, 0, 1:16:2] = 1
    i = np.arange(16)
    for q in range(N):
        t[q, 0, :, 0] = np.sum(np.abs(r[q, 0][:, o[q, 0, :, 0]] - h[q, 0, :, 0:1]), axis=0)
        t[q, 1, :, 0] = np.sum(np.abs(r[q, 1][:, o[q, 1, i, i]] - h[q, 1, :, :16]), axis=0) + (i % 2 == 0)
    return pack(h, w, t, m, o, r)
def setup_inputs_alike(rng):
    h, w, t, m, o, r = parts(rng)
    o[:, ::2] = rng.choice(np.array([0, R - 1, R // 2, 3]), (N, 4, 16, W)); o[:, 1::4] = o[:, 1::4, :1].copy()
    r[..., 0] = 0; r[..., R - 1] = 255
    h[..., 0::7] = 0; h[..., 1::7] = 255; h[..., 3::7] = r[..., R // 2][..., None]
    t[:, 2] = 1
    t[:, 4] = 4080; t[:, 4, 1::4] = rng.choice(np.array([4081, 4096]), (N, 4, 1)); o[:, 4, 1::4] = R - 1; o[:, 4, 12] = 3
    t[:, 6] = 0; o[:, 6, 1::4] = R // 2; o[:, 6, 0] = 3
    return pack(h, w, t, m, o, r)
def setup_inputs_spread(rng):
    h, w, t, m, o, r = parts(rng)
    h = (np.exp2(8 * rng.random((N, 8, 1, P))) * rng.random((N, 8, 16, P))).astype(np.int64)
    r = (np.exp2(8 * rng.random((N, 8, 1, R))) * rng.random((N, 8, 16, R))).astype(np.int64)
    w = np.minimum(np.exp2(8 * rng.random((N, 8, 16, 1))).astype(np.int64), 255)
    t = np.minimum(np.exp2(12 * rng.random((N, 8, 16, 1))).astype(np.int64), 4096)
    m = rng.random((N, 8, W)) < np.exp2(-8 * rng.random((N, 8, 1)))
    o = np.minimum((R * rng.random((N, 8, 16, W)) ** 3).astype(np.int64), R - 1)
    return pack(h, w, t, m, o, r)
def check_inputs(d):
    bad = []
    for k, hi in (("h0", 255), ("w", 255), ("th", 4096), ("marks", 1), ("owner", R - 1), ("hdr", 255)):
        v = np.asarray(d[k]).astype(np.float32)
        if not np.all((v >= 0) & (v <= hi) & (v == np.floor(v))): bad.append("range of " + k)
    if not np.all(np.asarray(d["marks"])[..., 0] == 1): bad.append("address 0 is a boundary")
    return bad
def reference(h0, w, th, marks, owner, hdr):
    h = h0.astype(np.float32).astype(np.int64).reshape(N, 8, 16, P); wt = w.astype(np.float32).astype(np.int64).reshape(N, 8, 16, 1)
    t = th.astype(np.int64).reshape(N, 8, 1, 16); m = marks > 0; o = owner.astype(np.int64).reshape(N, 8, 16, W)
    r = hdr.astype(np.float32).astype(np.int32).reshape(N, 8, 16, R)
    port = np.arange(P) & 15; slot = np.arange(16)
    for step in range(STEPS):
        u = np.add.reduce(wt * h, axis=2) & 4095
        x = ((((u * u) >> 5) + u) & (W - 16)) + port
        top = np.maximum.accumulate(np.where(m, np.arange(W), 0), axis=2)
        a = np.take_along_axis(top, x, 2); b = np.take_along_axis(top, (a - 1) & (W - 1), 2)
        ra = np.take_along_axis(o, a[:, :, None, :], 3); rb = np.take_along_axis(o, b[:, :, None, :], 3)
        new = []
        for q in range(N):
            ids = np.ascontiguousarray(ra[q].transpose(0, 2, 1)).reshape(8, 1, P * 16)
            v = np.take_along_axis(r[q], ids, 2).reshape(8, 16, P, 16)
            d = np.add.reduce(np.abs(v - h[q][..., None]), axis=1)
            n = np.where(d < t[q], slot, (d >> 2) & 15)
            e = np.zeros((8, P), np.int64) + port
            for hop in range(HOPS):
                e = np.take_along_axis(n, e[..., None], 2)[..., 0]
            done = np.take_along_axis(n, e[..., None], 2)[..., 0] == e
            ve = np.take_along_axis(v, e[:, None, :, None], 3)[..., 0]
            new.append(np.where(done[:, None, :], (h[q] + ve) >> 1, np.abs(h[q] - ve)))
            col = np.where(slot[None, :, None] == e[:, None, :], rb[q], ra[q])
            for g in range(8):
                lanes = np.flatnonzero(~done[g])
                xs, first = np.unique(x[q, g, lanes], return_index=True)
                o[q, g][:, xs] = col[g][:, lanes[first]]
                m[q, g, xs] = True
        h = np.roll(np.stack(new), SHIFT, axis=0)
    return {"yh": h.reshape(N, 128, P).astype(np.float32).astype(BF), "yo": o.reshape(N, 128, W).astype(np.float32), "ym": m.astype(np.float32)}

@@ -1,0 +1,345 @@
+from concourse.mybir import dt, AluOpType, AxisListType, ActivationFunctionType
+
+N, W, R, P, STEPS, SHIFT = 6, 1024, 8192, 512, 3, 2
+F32, BF, I32, U16 = "float32", "bfloat16", "int32", "uint16"
+SCRATCH = {}
+
+
+def sb(dtype, cols, names):
+    for n in names.split():
+        SCRATCH[n] = ("psum" if n[0] == "p" and n[1].isupper() else "sbuf", [128, cols], dtype)
+
+
+sb(BF, R, "hdrS")
+sb(I32, W, "owS mkS")
+sb(F32, W, "ow1 FW G NM MF WT Lm yoS ymS pM")
+sb(BF, W, "mkB")
+sb(F32, W + 128, "L")
+sb(F32, W + 16, "FB")
+sb(BF, 2048, "S WS U")
+sb(BF, 128, "ones rep8 bones idn idh idm tmpa tmpc")
+sb(BF, 16, "wS g8 g8w tmpb")
+sb(I32, 8, "thS pi ci gi")
+sb(F32, 8, "pcol ncol gcol coef thc frac")
+sb(F32, P, "jmod DIAG RST gm sc Wn Ws ra dr tt pU pD pK pE pX pA")
+sb(BF, P, "D Rn ab Q t2 hb0 hb1 hb2 hb3 hn0 hn1 hn2")
+sb(I32, P, "Bi")
+sb(F32, 32, "bpar b16 base dmp dump one32 ep0 thr0 xf xmd key kb t1 thr ge dq pr ep eqn win m1 off")
+sb(BF, 32, "e0 e done")
+sb(I32, 32, "ui um sq sh z zz pint qi q")
+sb(U16, 32, "XL XS PL OL SL")
+sb(BF, 256, "eq8")
+sb(F32, 256, "ls rst8")
+LOADS = ["marks", "w", "th", "owner", "h0", "hdr"]
+SEMAPHORES = ["V", "A", "T", "P"] + ["ld_" + n for n in LOADS] + ["arr%d" % k for k in range(STEPS)] \
+    + ["loc%d" % k for k in range(STEPS)] + ["st_yo0", "st_yo1", "st_ym", "st_yh"]
+TH_TOP = 4081.0
+HALF = 2041.0 / 4096.0
+
+
+def rank_program(g, core, T, topo):
+    rank = T.rank_of(core)
+    if rank is None:
+        return
+    A, AF = AluOpType, ActivationFunctionType
+    queues = {"V": g.vector, "A": g.scalar, "T": g.tensor, "P": g, "Y": g.sync}
+    known = {q: {} for q in queues}
+    clock = {}
+    count = {"V": 0, "A": 0, "T": 0, "P": 0}
+    total = {}
+    lastw, readers = {}, {}
+
+    def wait_for(q, deps):
+        best = {}
+        for s, v in deps:
+            if v > best.get(s, 0):
+                best[s] = v
+        todo = [(s, v) for s, v in best.items() if known[q].get(s, 0) < v]
+        todo = [d for d in todo if not any(o != d and clock[o].get(d[0], 0) >= d[1] for o in todo)]
+        for s, v in todo:
+            queues[q].wait_ge(T.sem[s], v)
+            for a, b in clock[(s, v)].items():
+                if b > known[q].get(a, 0):
+                    known[q][a] = b
+            known[q][s] = max(v, known[q].get(s, 0))
+
+    def deps_of(q, reads, writes):
+        d = []
+        for r in reads:
+            if r in lastw:
+                d.append(lastw[r])
+            if r[0] == "p" and r[1].isupper():
+                d += [(s, v) for s, v in readers.get(r, {}).items() if s != q]
+        for w in writes:
+            if w in lastw and lastw[w][0] != q:
+                d.append(lastw[w])
+            d += [(s, v) for s, v in readers.get(w, {}).items() if s != q]
+        return d
+
+    def note(s, v, reads, writes):
+        for r in reads:
+            readers.setdefault(r, {})[s] = v
+        for w in writes:
+            lastw[w] = (s, v)
+            readers[w] = {}
+
+    def op(q, fn, reads, writes):
+        wait_for(q, deps_of(q, reads, writes))
+        fn().then_inc(T.sem[q], 1)
+        count[q] += 1
+        total[q] = count[q]
+        clock[(q, count[q])] = dict(known[q])
+        note(q, count[q], reads, writes)
+
+    def dma(q, out, in_, sem, reads, writes):
+        wait_for(q, deps_of(sem, reads, writes))
+        queues[q].dma_start(out, in_).then_inc(T.sem[sem], 16)
+        total[sem] = 16
+        clock[(sem, 16)] = dict(known[q])
+        note(sem, 16, reads, writes)
+
+    vec = {"tt": g.vector.tensor_tensor, "ts": g.vector.tensor_scalar, "cp": g.vector.tensor_copy,
+           "scan": g.vector.tensor_tensor_scan, "tr": g.vector.transpose, "ms": g.vector.memset}
+
+    def V(name, reads, writes, *args):
+        op("V", lambda: vec[name](*args), reads.split(), writes.split())
+
+    def ACT(out, in_, func, reads, writes, bias=0.0, scale=1.0):
+        op("A", lambda: g.scalar.activation(out, in_, func, bias=bias, scale=scale), reads.split(), writes.split())
+
+    def MM(items, bank):
+        n = count["T"] + 1
+        for i, (out, l, r, st, sp, reads) in enumerate(items):
+            wait_for("T", deps_of("T", reads.split(), [bank]))
+            ins = g.tensor.matmul(out, l, r, st, sp)
+            if i == len(items) - 1:
+                ins.then_inc(T.sem["T"], 1)
+        count["T"] = n
+        total["T"] = n
+        clock[("T", n)] = dict(known["T"])
+        note("T", n, [r for it in items for r in it[5].split()], [bank])
+
+    def halves():
+        return [(hf, slice(hf * 512, hf * 512 + 512)) for hf in range(2)]
+
+    dma("Y", T.mkS[0:8, :], T.marks[:], "ld_marks", [], ["mkS"])
+    dma("Y", T.wS[:, 0:1], T.w[:], "ld_w", [], ["wS"])
+    dma("Y", T.thS[:, 0:1], T.th[:], "ld_th", [], ["thS"])
+    dma("Y", T.owS[:], T.owner[:], "ld_owner", [], ["owS"])
+    dma("Y", T.hb0[:], T.h0[:], "ld_h0", [], ["hb0"])
+    dma("Y", T.hdrS[:], T.hdr[:], "ld_hdr", [], ["hdrS"])
+
+    V("ms", "", "ones", T.ones[:], 1.0)
+    V("ms", "", "S", T.S[:], 0.0)
+    V("ms", "", "WS", T.WS[:], 0.0)
+    V("ms", "", "one32", T.one32[:], 1.0)
+    V("ms", "", "eq8", T.eq8[:], 0.0)
+
+    def iota(buf, name, pattern, base, cm):
+        op("P", lambda: g.iota(buf, pattern, base, cm, allow_small_or_imprecise_dtypes=True), [], [name])
+
+    def sel(out, in_, pattern, cmp, base, cm, reads, writes):
+        op("P", lambda: g.affine_select(out, in_, pattern, cmp, 0.0, base, cm), [reads], [writes])
+
+    op("P", lambda: g.iota(T.pi[:, 0:1], [[0, 1]], 0, 1), [], ["pi"])
+    sel(T.tmpc[0:8, :], T.ones[0:8, :], [[1, 128]], A.is_ge, 0, -16, "ones", "tmpc")
+    sel(T.rep8[0:8, :], T.tmpc[0:8, :], [[-1, 128]], A.is_ge, 15, 16, "tmpc", "rep8")
+    sel(T.tmpb[:, 0:8], T.ones[:, 0:8], [[-16, 8]], A.is_ge, 0, 1, "ones", "tmpb")
+    sel(T.g8[:, 0:8], T.tmpb[:, 0:8], [[16, 8]], A.is_ge, 15, -1, "tmpb", "g8")
+    iota(T.jmod[:], "jmod", [[0, 32], [1, 16]], 0, 0)
+    sel(T.tmpa[:], T.ones[:], [[-16, 8], [0, 16]], A.is_ge, 0, 1, "ones", "tmpa")
+    sel(T.bones[:], T.tmpa[:], [[16, 8], [0, 16]], A.is_ge, 15, -1, "tmpa", "bones")
+    sel(T.idn[:], T.ones[:], [[-1, 128]], A.is_equal, 0, 1, "ones", "idn")
+    iota(T.bpar[:], "bpar", [[0, 16], [1, 2]], 0, 0)
+    iota(T.b16[:], "b16", [[16, 32]], 0, 0)
+    iota(T.dmp[:], "dmp", [[0, 4], [16, 8]], W, 0)
+    iota(T.kb[:], "kb", [[W, 4], [0, 8]], 0, 0)
+    iota(T.rst8[:], "rst8", [[0, 32], [1, 8]], 0, 0)
+
+    V("cp", "mkS", "mkB", T.mkB[0:8, :], T.mkS[0:8, :])
+    for hf, cs in halves():
+        MM([(T.pM[:, cs], T.rep8[0:8, :], T.mkB[0:8, cs], True, True, "rep8 mkB")], "pM")
+    for hf, cs in halves():
+        ACT(T.NM[:, cs], T.pM[:, cs], AF.Identity, "pM", "NM%d" % hf, bias=1.0, scale=-1.0)
+
+    c1 = slice(0, 1)
+    V("ts", "pi", "ci", T.ci[:, c1], T.pi[:, c1], 15, None, A.bitwise_and)
+    V("ts", "pi", "gi", T.gi[:, c1], T.pi[:, c1], 4, 1, A.arith_shift_right, A.bitwise_and)
+    V("cp", "ci", "pcol", T.pcol[:, c1], T.ci[:, c1])
+    V("cp", "gi", "gcol", T.gcol[:, c1], T.gi[:, c1])
+    V("ts", "pcol", "ncol", T.ncol[:, c1], T.pcol[:, c1], -1.0, None, A.mult)
+    V("ts", "gcol", "coef", T.coef[:, c1], T.gcol[:, c1], 32.0, 496.0, A.mult, A.add)
+    V("cp", "thS", "thc", T.thc[:, c1], T.thS[:, c1])
+    V("ts", "thc", "frac", T.frac[:, c1], T.thc[:, c1], TH_TOP, 1.0 / 4096.0, A.min, A.mult)
+    V("ts", "g8 wS", "g8w", T.g8w[:, 0:8], T.g8[:, 0:8], T.wS[:, c1], None, A.mult)
+    for c in range(16):
+        V("cp", "g8w", "WS", T.WS[:, 129 * c:128 * (c + 1):16], T.g8w[:, 0:8])
+    pc = T.pcol[:, c1]
+    V("ts", "jmod pcol", "DIAG", T.DIAG[:], T.jmod[:], pc, None, A.is_equal)
+    V("ts", "jmod", "RST", T.RST[:], T.jmod[:], 0.0, None, A.not_equal)
+    for c in range(16):
+        ACT(T.S[:, 129 * c:128 * (c + 1):16], T.g8[:, 0:8], AF.Copy, "g8", "S")
+    for hf, cs in halves():
+        V("ts", "owS", "ow1", T.ow1[:, cs], T.owS[:, cs], 1.0, None, A.add)
+        V("tt", "ow1 pM", "L", T.L[:, cs], T.ow1[:, cs], T.pM[:, cs], A.mult)
+
+    def fill_F():
+        for hf, cs in halves():
+            V("scan", ("NM%d L" % hf) + (" FB" if hf else ""), "FB", T.FB[:, 8 + 512 * hf:520 + 512 * hf],
+              T.NM[:, cs], T.L[:, cs], T.FB[:, 519:520] if hf else 0.0, A.mult, A.add)
+
+    def fill_FW():
+        for hf, cs in halves():
+            ACT(T.FW[:, cs], T.FB[:, 8 + 512 * hf:520 + 512 * hf], AF.Copy, "FB", "FW", bias=-4097.0)
+
+    fill_F()
+    fill_FW()
+    V("ts", "bpar gcol", "m1", T.m1[:], T.bpar[:], T.gcol[:, c1], None, A.not_equal)
+    V("ts", "m1 coef", "off", T.off[:], T.m1[:], T.coef[:, c1], None, A.mult)
+    V("tt", "off b16", "base", T.base[:], T.off[:], T.b16[:], A.add)
+    V("ts", "base pcol", "ep0", T.ep0[:], T.base[:], pc, None, A.add)
+    V("ts", "one32 pcol", "e0", T.e0[:], T.one32[:], pc, None, A.mult)
+    V("ts", "one32 thc", "thr0", T.thr0[:], T.one32[:], T.thc[:, c1], None, A.mult)
+    V("ts", "dmp pcol", "dump", T.dump[:], T.dmp[:], pc, None, A.add)
+    V("ts", "idn", "idh", T.idh[:], T.idn[:], 0.5, None, A.mult)
+    V("ts", "idn", "idm", T.idm[:], T.idn[:], -1.0, None, A.mult)
+    V("ts", "rst8", "rst8", T.rst8[:], T.rst8[:], 0.0, None, A.not_equal)
+    for c in range(16):
+        V("ts", "bones DIAG", "U", T.U[:, 128 * c:128 * c + 128], T.bones[:], T.DIAG[:, c:c + 1], None, A.mult)
+
+    def blk(buf, c):
+        return buf[:, 128 * c:128 * c + 128]
+
+    def spread(src, name, bank):
+        MM([(T[bank][:, c::16], blk(T.U, c), src[:, 0:32], True, True, "U " + name) for c in range(16)], bank)
+
+    dst = T.cores[(rank + SHIFT) % N]
+    rid, pid, _ = topo.addr(dst)
+    emask = topo.mask(core, dst)
+    n_eng = len(topo.engines(core, dst))
+
+    for k in range(STEPS):
+        hN = "hb%d" % k
+        h = T[hN]
+        MM([(T.pU[:, 0:32], blk(T.WS, c), h[:, c::16], c == 0, c == 15, "WS " + hN) for c in range(16)], "pU")
+        V("cp", "pU", "ui", T.ui[:], T.pU[:, 0:32])
+        V("ts", "ui", "um", T.um[:], T.ui[:], 4095, None, A.bitwise_and)
+        V("tt", "um", "sq", T.sq[:], T.um[:], T.um[:], A.mult)
+        V("ts", "sq", "sh", T.sh[:], T.sq[:], 5, None, A.arith_shift_right)
+        V("tt", "sh um", "z", T.z[:], T.sh[:], T.um[:], A.add)
+        V("ts", "z", "zz", T.zz[:], T.z[:], W - 16, None, A.bitwise_and)
+        V("ts", "zz pcol", "XL", T.XL[:], T.zz[:], pc, None, A.add)
+        Fwin, FWwin = T.FB[:, 8:8 + W], T.FW[:, 0:W]
+        V("tt", "FB XL DIAG", "gm", T.gm[:], Fwin.indirect(T.XL[:]), T.DIAG[:], A.mult)
+        ACT(T.Wn[:], FWwin.indirect(T.XL[:]), AF.Identity, "FW XL frac", "Wn", bias=T.frac[:, c1])
+        V("ts", "zz pcol", "XS", T.XS[:, 0::2], T.zz[:, 1::2], pc, None, A.add)
+        V("ts", "zz pcol", "XS", T.XS[:, 1::2], T.zz[:, 0::2], pc, None, A.add)
+        ACT(T.Ws[:], FWwin.indirect(T.XS[:]), AF.Identity, "FW XS frac", "Ws", bias=T.frac[:, c1])
+        ACT(T.ra[:], Fwin.indirect(T.XL[:]), AF.Copy, "FB XL", "ra")
+        MM([(T.pX[:], T.idn[:], h[:], True, False, "idn " + hN)], "pX")
+
+        for hop in range(4):
+            e, eN = (T.e0, "e0") if hop == 0 else (T.e, "e")
+            ep, epN = (T.ep0, "ep0") if hop == 0 else (T.ep, "ep")
+            thr, thN = (T.thr0, "thr0") if hop == 0 else (T.thr, "thr")
+            if hop:
+                V("tt", "WT OL DIAG", "gm", T.gm[:], T.WT[:, 0:2 * P].indirect(T.OL[:]), T.DIAG[:], A.mult)
+            V("scan", "RST gm", "sc", T.sc[:], T.RST[:], T.gm[:], 0.0, A.mult, A.add)
+            if hop == 0:
+                V("ts", "sc", "PL", T.PL[:], T.sc[:, 15::16], -1.0, None, A.add)
+            else:
+                V("ts", "sc", "pint", T.pint[:], T.sc[:, 15::16], 4096.0 - HALF, None, A.add)
+                V("cp", "pint", "PL", T.PL[:], T.pint[:])
+            V("tt", "hdrS PL " + hN, "D", T.D[:], T.hdrS[:, 0:R].indirect(T.PL[:]), h[:], A.subtract)
+            V("ts", "D", "Rn", T.Rn[:], T.D[:], 0.0, -2.0, A.min, A.mult)
+            MM([(T.pD[:, 0:32], blk(T.S, c), T.D[:, c::16], c == 0, False, "S D") for c in range(16)]
+               + [(T.pD[:, 0:32], blk(T.S, c), T.Rn[:, c::16], False, c == 15, "S Rn") for c in range(16)], "pD")
+            if hop:
+                V("tt", "sc pint", "t1", T.t1[:], T.sc[:, 15::16], T.pint[:], A.subtract)
+            if hop == 0:
+                V("tr", "Wn", "WT", T.WT[:, 0:P], T.Wn[:])
+                V("tr", "Ws", "WT", T.WT[:, P:2 * P], T.Ws[:])
+            elif hop == 1:
+                V("cp", "FB", "FBw", T.FB[:, 7:8], T.FB[:, 7 + W:8 + W])
+                V("ts", "t1", "thr", T.thr[:], T.t1[:], 4096.0, 4096.0, A.add, A.mult)
+                V("tt", "FB FBw pM", "MF", T.MF[:], T.FB[:, 7:7 + W], T.pM[:], A.mult)
+            elif hop == 2:
+                V("ts", "zz pcol", "xf", T.xf[:], T.zz[:], pc, None, A.add)
+                V("ts", "t1", "thr", T.thr[:], T.t1[:], 4096.0, 4096.0, A.add, A.mult)
+                V("scan", "NM0 NM1 MF", "G", T.G[:], T.NM[:], T.MF[:], 0.0, A.mult, A.add)
+                V("tt", "xf kb", "key", T.key[:], T.xf[:], T.kb[:], A.add)
+                V("tt", "xf dump", "xmd", T.xmd[:], T.xf[:], T.dump[:], A.subtract)
+            else:
+                MM([(T.pX[:], T.idh[:], T.D[:], False, True, "idh D")], "pX")
+                MM([(T.pA[:], T.idn[:], T.D[:], True, False, "idn D"),
+                    (T.pA[:], T.idn[:], T.Rn[:], False, True, "idn Rn")], "pA")
+                V("tt", "G XL ra", "dr", T.dr[:], T.G[:, 0:W].indirect(T.XL[:]), T.ra[:], A.subtract)
+                V("ts", "t1", "thr", T.thr[:], T.t1[:], 4096.0, 4096.0, A.add, A.mult)
+                for j in range(1, 8):
+                    V("tt", "key", "eq8", T.eq8[:, 9 * j::8], T.key[:, j:32], T.key[:, 0:32 - j], A.is_equal)
+            V("cp", "pD", "qi", T.qi[:], T.pD[:, 0:32])
+            V("tt", "pD " + thN, "ge", T.ge[:], T.pD[:, 0:32], thr[:], A.is_ge if hop < 3 else A.is_lt)
+            V("ts", "qi", "q", T.q[:], T.qi[:], 2, 15, A.arith_shift_right, A.bitwise_and)
+            if hop < 3:
+                V("tt", "q " + eN, "dq", T.dq[:], T.q[:], e[:], A.subtract)
+                V("tt", "dq ge", "pr", T.pr[:], T.dq[:], T.ge[:], A.mult)
+                V("tt", "pr " + epN, "ep", T.ep[:], T.pr[:], ep[:], A.add)
+                V("tt", "pr " + eN, "e", T.e[:], T.pr[:], e[:], A.add)
+                V("cp", "ep", "OL", T.OL[:], T.ep[:])
+                if hop == 2:
+                    spread(T.e, "e", "pE")
+                    ACT(T.ab[:], T.pE[:], AF.Abs, "pE ncol", "ab", bias=T.ncol[:, c1])
+                    ACT(T.pK[:], T.ab[:], AF.Relu, "ab", "pK", bias=1.0, scale=-1.0)
+            else:
+                V("tt", "q e", "eqn", T.eqn[:], T.q[:], T.e[:], A.is_equal)
+                V("tt", "ge eqn", "done", T.done[:], T.ge[:], T.eqn[:], A.max)
+
+        spread(T.done, "done", "pE")
+        MM([(T.pU[:, 0:256], T.idn[:], T.eq8[:], True, False, "idn eq8")]
+           + [(T.pU[:, 9 * j:256:8], T.idm[:], T.done[:, 0:32 - j], False, j == 7, "idm done")
+              for j in range(1, 8)], "pU")
+        V("ts", "done", "win", T.win[:], T.done[:], 0.0, None, A.is_equal)
+        V("ts", "pX", "Bi", T.Bi[:], T.pX[:], -0.25, None, A.add)
+        V("tt", "Bi pA", "Q", T.Q[:], T.Bi[:], T.pA[:], A.subtract)
+        V("tt", "Q pE", "t2", T.t2[:], T.Q[:], T.pE[:], A.mult)
+        hn = "hn%d" % k
+        V("tt", "t2 pA", hn, T[hn][:], T.t2[:], T.pA[:], A.add)
+        wait_for("P", deps_of("P", [hn], []))
+        arr, loc, nxt = "arr%d" % k, "loc%d" % k, "hb%d" % (k + 1)
+        g.remote_dma(T[nxt][:], T[hn][:], T.sem[arr], T.sem[loc], pid, rid, emask)
+        for s in (arr, loc):
+            total[s] = n_eng
+            clock[(s, n_eng)] = {}
+        lastw[nxt] = (arr, n_eng)
+
+        V("scan", "rst8 pU", "ls", T.ls[:], T.rst8[:], T.pU[:, 0:256], 0.0, A.mult, A.max)
+        V("tt", "dr pK", "tt", T.tt[:], T.dr[:], T.pK[:], A.mult)
+        V("tt", "win ls", "win", T.win[:], T.win[:], T.ls[:, 7::8], A.is_gt)
+        V("tt", "win xmd", "m1", T.m1[:], T.win[:], T.xmd[:], A.mult)
+        V("tt", "m1 dump", "off", T.off[:], T.m1[:], T.dump[:], A.add)
+        V("cp", "off", "SL", T.SL[:], T.off[:])
+        for j in reversed(range(4)):
+            cs = slice(128 * j, 128 * j + 128)
+            V("tt", "SL tt ra L", "L", T.L[:, 0:W + 128].indirect(T.SL[:, 8 * j:8 * j + 8]),
+              T.tt[:, cs], T.ra[:, cs], A.add)
+        if k < STEPS - 1:
+            for hf, cs in halves():
+                ACT(T.NM[:, cs], T.L[:, cs], AF.Relu, "L", "NM%d" % hf, bias=1.0, scale=-1.0)
+            fill_F()
+            for hf, cs in halves():
+                ACT(T.pM[:, cs], T.L[:, cs], AF.Sign, "L", "pM")
+            fill_FW()
+
+    for hf, cs in halves():
+        bank, pm = ("pX", "pU") if hf == 0 else ("pA", "pD")
+        ACT(T[pm][:], T.L[:, cs], AF.Relu, "L", pm, bias=1.0, scale=-1.0)
+        ACT(T.Lm[:, cs], T.L[:, cs], AF.Copy, "L", "Lm%d" % hf, bias=-1.0)
+        V("tt", "ow1 " + pm, bank, T[bank][:], T.ow1[:, cs], T[pm][:], A.mult)
+        V("tt", ("Lm%d " % hf) + bank, "yoS%d" % hf, T.yoS[:, cs], T.Lm[:, cs], T[bank][:], A.add)
+    ACT(T.ymS[:], T.L[:, 0:W], AF.Sign, "L", "ymS")
+    for hf, cs in halves():
+        dma("A", T.yo[:, cs], T.yoS[:, cs], "st_yo%d" % hf, ["yoS%d" % hf], [])
+    dma("A", T.ym[:], T.ymS[0::16, :], "st_ym", ["ymS"], [])
+    dma("Y", T.yh[:], T["hb%d" % STEPS][:], "st_yh", ["hb%d" % STEPS], [])
+    for s, v in total.items():
+        g.wait_ge(T.sem[s], v)

@@ -12,29 +12,31 @@ def sb(dtype, cols, names):
 
 sb(BF, R, "hdrS")
 sb(I32, W, "owS mkS")
-sb(F32, W, "ow1 FW G NM MF WT Lm yoS ymS pM")
+sb(F32, W, "o4 o5 FW G NM MF AL sg yoS ymS pM Wg WT")
 sb(BF, W, "mkB")
-sb(F32, W + 128, "L")
+sb(F32, W + 128, "TB")
 sb(F32, W + 16, "FB")
 sb(BF, 2048, "S WS U")
 sb(BF, 128, "ones rep8 bones idn idh idm tmpa tmpc")
 sb(BF, 16, "wS g8 g8w tmpb")
 sb(I32, 8, "thS pi ci gi")
-sb(F32, 8, "pcol ncol gcol coef thc frac")
-sb(F32, P, "jmod DIAG RST gm sc Wn Ws ra dr tt pU pD pK pE pX pA")
-sb(BF, P, "D Rn ab Q t2 hb0 hb1 hb2 hb3 hn0 hn1 hn2")
-sb(I32, P, "Bi")
-sb(F32, 32, "bpar b16 base dmp dump one32 ep0 thr0 xf xmd key kb t1 thr ge dq pr ep eqn win m1 off")
-sb(BF, 32, "e0 e done")
-sb(I32, 32, "ui um sq sh z zz pint qi q")
-sb(U16, 32, "XL XS PL OL SL")
+sb(F32, 8, "pcol ncol gcol coef thc fth")
+sb(F32, 256, "jmod DIAG RST rst8 ls")
+sb(F32, 32, "bpar b16 ne nb base ep0 dmp dump pmd kb one32 e0 thr0 xmd p4 thr ge dq pr ep eqn win m1 off")
+sb(F32, P, "pU pD pE pK pX pB gm sc ra dr tt y")
+sb(BF, P, "D Rn ab Q hb0 hb1 hb2 hb3 hn0 hn1 hn2")
 sb(BF, 256, "eq8")
-sb(F32, 256, "ls rst8")
-LOADS = ["marks", "w", "th", "owner", "h0", "hdr"]
-SEMAPHORES = ["V", "A", "T", "P"] + ["ld_" + n for n in LOADS] + ["arr%d" % k for k in range(STEPS)] \
-    + ["loc%d" % k for k in range(STEPS)] + ["st_yo0", "st_yo1", "st_ym", "st_yh"]
+sb(I32, 32, "ui um uo sq zz qi q")
+sb(BF, 32, "key e done")
+sb(U16, 64, "XL PL OL SL")
+LOADS = ["marks", "owner", "w", "th", "h0", "hdr"]
+SEMAPHORES = ["V", "A", "T", "P"] + ["ld_" + n for n in LOADS] \
+    + [n + str(k) for n in ("arr", "loc") for k in range(STEPS)] + ["st_yo0", "st_yo1", "st_ym", "st_yh"]
 TH_TOP = 4081.0
 HALF = 2041.0 / 4096.0
+BIG = 8388608.0
+CYC, PE, WAKE, DMA, SEND, FLY = 0.83, 0.6, 80, 2000, 1200, 2800
+LOOK, TOL = 300, 60
 
 
 def rank_program(g, core, T, topo):
@@ -43,126 +45,213 @@ def rank_program(g, core, T, topo):
         return
     A, AF = AluOpType, ActivationFunctionType
     queues = {"V": g.vector, "A": g.scalar, "T": g.tensor, "P": g, "Y": g.sync}
-    known = {q: {} for q in queues}
-    clock = {}
-    count = {"V": 0, "A": 0, "T": 0, "P": 0}
-    total = {}
-    lastw, readers = {}, {}
+    nodes = []
 
-    def wait_for(q, deps):
-        best = {}
-        for s, v in deps:
-            if v > best.get(s, 0):
-                best[s] = v
-        todo = [(s, v) for s, v in best.items() if known[q].get(s, 0) < v]
-        todo = [d for d in todo if not any(o != d and clock[o].get(d[0], 0) >= d[1] for o in todo)]
-        for s, v in todo:
-            queues[q].wait_ge(T.sem[s], v)
-            for a, b in clock[(s, v)].items():
-                if b > known[q].get(a, 0):
-                    known[q][a] = b
-            known[q][s] = max(v, known[q].get(s, 0))
+    def node(q, emit, reads, writes, cost, lat=0.0, sem=None, early=0.0):
+        nodes.append({"q": q, "emit": emit, "r": reads, "w": writes, "cost": cost, "lat": lat, "sem": sem or (q, 1),
+                      "early": early})
 
-    def deps_of(q, reads, writes):
-        d = []
-        for r in reads:
-            if r in lastw:
-                d.append(lastw[r])
-            if r[0] == "p" and r[1].isupper():
-                d += [(s, v) for s, v in readers.get(r, {}).items() if s != q]
-        for w in writes:
-            if w in lastw and lastw[w][0] != q:
-                d.append(lastw[w])
-            d += [(s, v) for s, v in readers.get(w, {}).items() if s != q]
-        return d
-
-    def note(s, v, reads, writes):
-        for r in reads:
-            readers.setdefault(r, {})[s] = v
-        for w in writes:
-            lastw[w] = (s, v)
-            readers[w] = {}
-
-    def op(q, fn, reads, writes):
-        wait_for(q, deps_of(q, reads, writes))
-        fn().then_inc(T.sem[q], 1)
-        count[q] += 1
-        total[q] = count[q]
-        clock[(q, count[q])] = dict(known[q])
-        note(q, count[q], reads, writes)
-
-    def dma(q, out, in_, sem, reads, writes):
-        wait_for(q, deps_of(sem, reads, writes))
-        queues[q].dma_start(out, in_).then_inc(T.sem[sem], 16)
-        total[sem] = 16
-        clock[(sem, 16)] = dict(known[q])
-        note(sem, 16, reads, writes)
+    def op(q, fn, reads, writes, cost):
+        node(q, [(fn, reads)], reads, writes, cost)
 
     vec = {"tt": g.vector.tensor_tensor, "ts": g.vector.tensor_scalar, "cp": g.vector.tensor_copy,
            "scan": g.vector.tensor_tensor_scan, "tr": g.vector.transpose, "ms": g.vector.memset}
 
-    def V(name, reads, writes, *args):
-        op("V", lambda: vec[name](*args), reads.split(), writes.split())
+    def V(name, reads, writes, *args, c=64):
+        op("V", lambda: vec[name](*args), reads.split(), writes.split(), c * CYC)
 
-    def ACT(out, in_, func, reads, writes, bias=0.0, scale=1.0):
-        op("A", lambda: g.scalar.activation(out, in_, func, bias=bias, scale=scale), reads.split(), writes.split())
+    def ACT(out, in_, func, reads, writes, c=512, bias=0.0, scale=1.0):
+        op("A", lambda: g.scalar.activation(out, in_, func, bias=bias, scale=scale), reads.split(), writes.split(),
+           c * CYC)
 
-    def MM(items, bank):
-        n = count["T"] + 1
-        for i, (out, l, r, st, sp, reads) in enumerate(items):
-            wait_for("T", deps_of("T", reads.split(), [bank]))
-            ins = g.tensor.matmul(out, l, r, st, sp)
-            if i == len(items) - 1:
-                ins.then_inc(T.sem["T"], 1)
-        count["T"] = n
-        total["T"] = n
-        clock[("T", n)] = dict(known["T"])
-        note("T", n, [r for it in items for r in it[5].split()], [bank])
+    def MM(items, bank, n=64):
+        emit = [((lambda it=it: g.tensor.matmul(it[0], it[1], it[2], it[3], it[4])), it[5].split()) for it in items]
+        node("T", emit, [r for e in emit for r in e[1]], [bank], len(items) * n * PE)
 
-    def halves():
-        return [(hf, slice(hf * 512, hf * 512 + 512)) for hf in range(2)]
+    def dma(out, in_, sem, reads, writes, lat=DMA, early=0.0):
+        node("Y", [((lambda: g.sync.dma_start(out, in_)), reads)], reads, writes, 60, lat, (sem, 16), early)
 
-    dma("Y", T.mkS[0:8, :], T.marks[:], "ld_marks", [], ["mkS"])
-    dma("Y", T.wS[:, 0:1], T.w[:], "ld_w", [], ["wS"])
-    dma("Y", T.thS[:, 0:1], T.th[:], "ld_th", [], ["thS"])
-    dma("Y", T.owS[:], T.owner[:], "ld_owner", [], ["owS"])
-    dma("Y", T.hb0[:], T.h0[:], "ld_h0", [], ["hb0"])
-    dma("Y", T.hdrS[:], T.hdr[:], "ld_hdr", [], ["hdrS"])
+    def ga(n):
+        return 60 + 1.5 * n
 
-    V("ms", "", "ones", T.ones[:], 1.0)
-    V("ms", "", "S", T.S[:], 0.0)
-    V("ms", "", "WS", T.WS[:], 0.0)
-    V("ms", "", "one32", T.one32[:], 1.0)
-    V("ms", "", "eq8", T.eq8[:], 0.0)
+    def is_bank(r):
+        return r[0] == "p" and r[1].isupper()
 
-    def iota(buf, name, pattern, base, cm):
-        op("P", lambda: g.iota(buf, pattern, base, cm, allow_small_or_imprecise_dtypes=True), [], [name])
+    def schedule():
+        lastw, rd = {}, {}
+        preds = []
+        for i, d in enumerate(nodes):
+            ps = set()
+            for r in d["r"]:
+                if r in lastw:
+                    ps.add(lastw[r])
+                if is_bank(r):
+                    ps.update(rd.get(r, ()))
+            for w in d["w"]:
+                if w in lastw:
+                    ps.add(lastw[w])
+                ps.update(rd.get(w, ()))
+            ps.discard(i)
+            preds.append(ps)
+            for r in d["r"]:
+                rd.setdefault(r, []).append(i)
+            for w in d["w"]:
+                lastw[w] = i
+                rd[w] = []
+        n = len(nodes)
+        succ = [[] for _ in range(n)]
+        for i, ps in enumerate(preds):
+            for p in ps:
+                succ[p].append(i)
+        prio = [0.0] * n
+        for i in range(n - 1, -1, -1):
+            d = nodes[i]
+            prio[i] = d["cost"] + d["lat"] + max([prio[s] + WAKE for s in succ[i]] + [0.0])
+        left = [len(p) for p in preds]
+        avail = [0.0] * n
+        ready = [i for i in range(n) if not left[i]]
+        free = {q: 0.0 for q in queues}
+        order = []
+        while ready:
+            st = {i: max(free[nodes[i]["q"]], avail[i]) for i in ready}
+            t = min(st.values())
+            q = nodes[min(ready, key=lambda i: (st[i], i))]["q"]
+            cand = sorted([i for i in ready if nodes[i]["q"] == q and st[i] <= t + LOOK],
+                          key=lambda j: (-prio[j] - nodes[j]["early"], j))
+            i = cand[0]
+            for j in cand:
+                if st[j] <= t + 30 and t + nodes[j]["cost"] <= st[i] + TOL:
+                    i = j
+                    break
+            d = nodes[i]
+            ready.remove(i)
+            order.append(i)
+            free[q] = st[i] + d["cost"]
+            for s in succ[i]:
+                avail[s] = max(avail[s], free[q] + d["lat"] + WAKE)
+                left[s] -= 1
+                if not left[s]:
+                    ready.append(s)
+        return order
 
-    def sel(out, in_, pattern, cmp, base, cm, reads, writes):
-        op("P", lambda: g.affine_select(out, in_, pattern, cmp, 0.0, base, cm), [reads], [writes])
+    def issue(order):
+        known = {q: {} for q in queues}
+        clock, total, lastw, rd = {}, {}, {}, {}
 
-    op("P", lambda: g.iota(T.pi[:, 0:1], [[0, 1]], 0, 1), [], ["pi"])
-    sel(T.tmpc[0:8, :], T.ones[0:8, :], [[1, 128]], A.is_ge, 0, -16, "ones", "tmpc")
-    sel(T.rep8[0:8, :], T.tmpc[0:8, :], [[-1, 128]], A.is_ge, 15, 16, "tmpc", "rep8")
-    sel(T.tmpb[:, 0:8], T.ones[:, 0:8], [[-16, 8]], A.is_ge, 0, 1, "ones", "tmpb")
-    sel(T.g8[:, 0:8], T.tmpb[:, 0:8], [[16, 8]], A.is_ge, 15, -1, "tmpb", "g8")
-    iota(T.jmod[:], "jmod", [[0, 32], [1, 16]], 0, 0)
-    sel(T.tmpa[:], T.ones[:], [[-16, 8], [0, 16]], A.is_ge, 0, 1, "ones", "tmpa")
-    sel(T.bones[:], T.tmpa[:], [[16, 8], [0, 16]], A.is_ge, 15, -1, "tmpa", "bones")
-    sel(T.idn[:], T.ones[:], [[-1, 128]], A.is_equal, 0, 1, "ones", "idn")
-    iota(T.bpar[:], "bpar", [[0, 16], [1, 2]], 0, 0)
-    iota(T.b16[:], "b16", [[16, 32]], 0, 0)
-    iota(T.dmp[:], "dmp", [[0, 4], [16, 8]], W, 0)
-    iota(T.kb[:], "kb", [[W, 4], [0, 8]], 0, 0)
-    iota(T.rst8[:], "rst8", [[0, 32], [1, 8]], 0, 0)
+        def wait_for(q, deps):
+            best = {}
+            for s, v in deps:
+                best[s] = max(v, best.get(s, 0))
+            todo = [(s, v) for s, v in best.items() if known[q].get(s, 0) < v]
+            todo = [d for d in todo if not any(o != d and clock[o].get(d[0], 0) >= d[1] for o in todo)]
+            for s, v in todo:
+                queues[q].wait_ge(T.sem[s], v)
+                for a, b in clock[(s, v)].items():
+                    known[q][a] = max(b, known[q].get(a, 0))
+                known[q][s] = max(v, known[q].get(s, 0))
 
-    V("cp", "mkS", "mkB", T.mkB[0:8, :], T.mkS[0:8, :])
-    for hf, cs in halves():
-        MM([(T.pM[:, cs], T.rep8[0:8, :], T.mkB[0:8, cs], True, True, "rep8 mkB")], "pM")
-    for hf, cs in halves():
-        ACT(T.NM[:, cs], T.pM[:, cs], AF.Identity, "pM", "NM%d" % hf, bias=1.0, scale=-1.0)
+        for i in order:
+            d = nodes[i]
+            q, (sem, inc) = d["q"], d["sem"]
+            ins = None
+            for j, (fn, reads) in enumerate(d["emit"]):
+                deps = []
+                for r in reads:
+                    if r in lastw:
+                        deps.append(lastw[r])
+                    if is_bank(r):
+                        deps += [x for x in rd.get(r, {}).items() if x[0] != sem]
+                for w in d["w"] if j == 0 else []:
+                    if w in lastw and lastw[w][0] != sem:
+                        deps.append(lastw[w])
+                    deps += [x for x in rd.get(w, {}).items() if x[0] != sem]
+                wait_for(q, deps)
+                ins = fn()
+            if inc == 0:
+                key, rkey = d["remote"]
+                for s, v in (key, rkey):
+                    total[s] = v
+                    clock[(s, v)] = {}
+            else:
+                ins.then_inc(T.sem[sem], inc)
+                total[sem] = total.get(sem, 0) + inc
+                clock[(sem, total[sem])] = dict(known[q])
+                key = rkey = (sem, total[sem])
+            for r in d["r"]:
+                rd.setdefault(r, {})[rkey[0]] = rkey[1]
+            for w in d["w"]:
+                lastw[w] = key
+                rd[w] = {}
+        for s, v in total.items():
+            g.wait_ge(T.sem[s], v)
+
+    def halves(n=512):
+        return [(hf, slice(hf * n, hf * n + n)) for hf in range(2)]
 
     c1 = slice(0, 1)
+    dma(T.mkS[0:8, :], T.marks[:], "ld_marks", [], ["mkS"], early=9e6)
+    dma(T.owS[:], T.owner[:], "ld_owner", [], ["owS"], 4000, early=8e6)
+    dma(T.wS[:, c1], T.w[:], "ld_w", [], ["wS"], 5000, early=7e6)
+    dma(T.thS[:, c1], T.th[:], "ld_th", [], ["thS"], 5000, early=6e6)
+    dma(T.hb0[:], T.h0[:], "ld_h0", [], ["hb0"], 5500, early=5e6)
+    dma(T.hdrS[:], T.hdr[:], "ld_hdr", [], ["hdrS"], 12000)
+
+    def iota(buf, name, pattern, base, cm, c):
+        op("P", lambda: g.iota(buf, pattern, base, cm, allow_small_or_imprecise_dtypes=True), [], [name], 150 + 2 * c)
+
+    def sel(out, in_, pattern, cmp, base, cm, reads, writes, c):
+        op("P", lambda: g.affine_select(out, in_, pattern, cmp, 0.0, base, cm), [reads], [writes], 170 + 2 * c)
+
+    V("ms", "", "ones", T.ones[:], 1.0)
+    op("P", lambda: g.iota(T.pi[:, c1], [[0, 1]], 0, 1), [], ["pi"], 150)
+    sel(T.tmpc[0:8, :], T.ones[0:8, :], [[1, 128]], A.is_ge, 0, -16, "ones", "tmpc", 128)
+    sel(T.rep8[0:8, :], T.tmpc[0:8, :], [[-1, 128]], A.is_ge, 15, 16, "tmpc", "rep8", 128)
+    V("cp", "mkS", "mkB", T.mkB[0:8, :], T.mkS[0:8, :], c=1024)
+    for hf, cs in halves():
+        MM([(T.pM[:, cs], T.rep8[0:8, :], T.mkB[0:8, cs], True, True, "rep8 mkB")], "pM", 512)
+    for hf, cs in halves():
+        sg = ("pE", "pK")[hf]
+        ACT(T[sg][:], T.pM[:, cs], AF.Copy, "pM", sg, bias=-1.0, scale=2.0)
+        V("ts", "owS", "o4_%d" % hf, T.o4[:, cs], T.owS[:, cs], 4096.0, None, A.add, c=512)
+        V("tt", "o4_%d %s" % (hf, sg), "o5_%d" % hf, T.o5[:, cs], T.o4[:, cs], T[sg][:], A.mult, c=512)
+        ACT(T.TB[:, cs], T.o5[:, cs], AF.Copy, "o5_%d" % hf, "TB", bias=-4096.0)
+
+    def tables(first):
+        for hf, cs in halves():
+            ACT(T.AL[:, cs], T.TB[:, cs], AF.Abs, "TB", "AL%d" % hf)
+        for hf, cs in halves():
+            fs = slice(8 + 512 * hf, 520 + 512 * hf)
+            V("scan", ("AL%d TB" % hf) + (" FB" if hf else ""), "FB", T.FB[:, fs],
+              T.AL[:, cs], T.TB[:, cs], T.FB[:, 519:520] if hf else 0.0, A.min, A.max, c=512)
+        for hf, cs in halves():
+            fs = slice(8 + 512 * hf, 520 + 512 * hf)
+            ACT(T.FW[:, cs], T.FB[:, fs], AF.Copy, "FB", "FW", bias=-16777216.0, scale=4096.0)
+        if first:
+            ACT(T.NM[:], T.pM[:], AF.Copy, "pM", "NM", 1024, bias=1.0, scale=-1.0)
+        else:
+            ACT(T.sg[:], T.TB[:, 0:W], AF.Sign, "TB", "sg", 1024, bias=0.5)
+            ACT(T.pM[:], T.sg[:], AF.Relu, "sg", "pM", 1024)
+            ACT(T.NM[:], T.sg[:], AF.Relu, "sg", "NM", 1024, scale=-1.0)
+        V("cp", "FB", "FBw", T.FB[:, 7:8], T.FB[:, 7 + W:8 + W])
+        V("tt", "FB FBw pM", "MF0", T.MF[:, 0:512], T.FB[:, 7:519], T.pM[:, 0:512], A.mult, c=512)
+        V("tt", "FB pM", "MF1", T.MF[:, 512:], T.FB[:, 519:7 + W], T.pM[:, 512:], A.mult, c=512)
+        V("scan", "NM MF0", "G", T.G[:, 0:512], T.NM[:, 0:512], T.MF[:, 0:512], 0.0, A.mult, A.add, c=512)
+        V("scan", "NM MF1 G", "G", T.G[:, 512:], T.NM[:, 512:], T.MF[:, 512:], T.G[:, 511:512], A.mult, A.add, c=512)
+
+    sel(T.tmpb[:, 0:8], T.ones[:, 0:8], [[-16, 8]], A.is_ge, 0, 1, "ones", "tmpb", 8)
+    sel(T.g8[:, 0:8], T.tmpb[:, 0:8], [[16, 8]], A.is_ge, 15, -1, "tmpb", "g8", 8)
+    iota(T.jmod[:], "jmod", [[0, 16], [1, 16]], 0, 0, 256)
+    sel(T.tmpa[:], T.ones[:], [[-16, 8], [0, 16]], A.is_ge, 0, 1, "ones", "tmpa", 128)
+    sel(T.bones[:], T.tmpa[:], [[16, 8], [0, 16]], A.is_ge, 15, -1, "tmpa", "bones", 128)
+    sel(T.idn[:], T.ones[:], [[-1, 128]], A.is_equal, 0, 1, "ones", "idn", 128)
+    iota(T.bpar[:], "bpar", [[0, 16], [1, 2]], 0, 0, 32)
+    iota(T.b16[:], "b16", [[16, 32]], 0, 0, 32)
+    iota(T.dmp[:], "dmp", [[0, 4], [16, 8]], W, 0, 32)
+    iota(T.kb[:], "kb", [[0, 2], [W, 2], [0, 8]], W, 0, 32)
+    iota(T.rst8[:], "rst8i", [[0, 32], [1, 8]], 0, 0, 256)
+    V("ms", "", "S", T.S[:], 0.0, c=1024)
+    V("ms", "", "WS", T.WS[:], 0.0, c=1024)
+    V("ms", "", "one32", T.one32[:], 1.0)
     V("ts", "pi", "ci", T.ci[:, c1], T.pi[:, c1], 15, None, A.bitwise_and)
     V("ts", "pi", "gi", T.gi[:, c1], T.pi[:, c1], 4, 1, A.arith_shift_right, A.bitwise_and)
     V("cp", "ci", "pcol", T.pcol[:, c1], T.ci[:, c1])
@@ -170,53 +259,43 @@ def rank_program(g, core, T, topo):
     V("ts", "pcol", "ncol", T.ncol[:, c1], T.pcol[:, c1], -1.0, None, A.mult)
     V("ts", "gcol", "coef", T.coef[:, c1], T.gcol[:, c1], 32.0, 496.0, A.mult, A.add)
     V("cp", "thS", "thc", T.thc[:, c1], T.thS[:, c1])
-    V("ts", "thc", "frac", T.frac[:, c1], T.thc[:, c1], TH_TOP, 1.0 / 4096.0, A.min, A.mult)
+    V("ts", "thc", "fth", T.fth[:, c1], T.thc[:, c1], TH_TOP, None, A.min)
     V("ts", "g8 wS", "g8w", T.g8w[:, 0:8], T.g8[:, 0:8], T.wS[:, c1], None, A.mult)
     for c in range(16):
         V("cp", "g8w", "WS", T.WS[:, 129 * c:128 * (c + 1):16], T.g8w[:, 0:8])
-    pc = T.pcol[:, c1]
-    V("ts", "jmod pcol", "DIAG", T.DIAG[:], T.jmod[:], pc, None, A.is_equal)
-    V("ts", "jmod", "RST", T.RST[:], T.jmod[:], 0.0, None, A.not_equal)
     for c in range(16):
-        ACT(T.S[:, 129 * c:128 * (c + 1):16], T.g8[:, 0:8], AF.Copy, "g8", "S")
-    for hf, cs in halves():
-        V("ts", "owS", "ow1", T.ow1[:, cs], T.owS[:, cs], 1.0, None, A.add)
-        V("tt", "ow1 pM", "L", T.L[:, cs], T.ow1[:, cs], T.pM[:, cs], A.mult)
-
-    def fill_F():
-        for hf, cs in halves():
-            V("scan", ("NM%d L" % hf) + (" FB" if hf else ""), "FB", T.FB[:, 8 + 512 * hf:520 + 512 * hf],
-              T.NM[:, cs], T.L[:, cs], T.FB[:, 519:520] if hf else 0.0, A.mult, A.add)
-
-    def fill_FW():
-        for hf, cs in halves():
-            ACT(T.FW[:, cs], T.FB[:, 8 + 512 * hf:520 + 512 * hf], AF.Copy, "FB", "FW", bias=-4097.0)
-
-    fill_F()
-    fill_FW()
-    V("ts", "bpar gcol", "m1", T.m1[:], T.bpar[:], T.gcol[:, c1], None, A.not_equal)
-    V("ts", "m1 coef", "off", T.off[:], T.m1[:], T.coef[:, c1], None, A.mult)
-    V("tt", "off b16", "base", T.base[:], T.off[:], T.b16[:], A.add)
+        ACT(T.S[:, 129 * c:128 * (c + 1):16], T.g8[:, 0:8], AF.Copy, "g8", "S", 64)
+    pc = T.pcol[:, c1]
+    V("ts", "jmod pcol", "DIAG", T.DIAG[:], T.jmod[:], pc, None, A.is_equal, c=256)
+    V("ts", "jmod", "RST", T.RST[:], T.jmod[:], 0.0, None, A.not_equal, c=256)
+    V("ts", "bpar gcol", "ne", T.ne[:], T.bpar[:], T.gcol[:, c1], None, A.not_equal)
+    V("ts", "ne coef", "nb", T.nb[:], T.ne[:], T.coef[:, c1], None, A.mult)
+    V("tt", "nb b16", "base", T.base[:], T.nb[:], T.b16[:], A.add)
     V("ts", "base pcol", "ep0", T.ep0[:], T.base[:], pc, None, A.add)
     V("ts", "one32 pcol", "e0", T.e0[:], T.one32[:], pc, None, A.mult)
     V("ts", "one32 thc", "thr0", T.thr0[:], T.one32[:], T.thc[:, c1], None, A.mult)
     V("ts", "dmp pcol", "dump", T.dump[:], T.dmp[:], pc, None, A.add)
+    V("ts", "dmp", "pmd", T.pmd[:], T.dmp[:], -1.0, None, A.mult)
     V("ts", "idn", "idh", T.idh[:], T.idn[:], 0.5, None, A.mult)
     V("ts", "idn", "idm", T.idm[:], T.idn[:], -1.0, None, A.mult)
-    V("ts", "rst8", "rst8", T.rst8[:], T.rst8[:], 0.0, None, A.not_equal)
+    V("ts", "rst8i", "rst8", T.rst8[:], T.rst8[:], 0.0, None, A.not_equal, c=256)
     for c in range(16):
         V("ts", "bones DIAG", "U", T.U[:, 128 * c:128 * c + 128], T.bones[:], T.DIAG[:, c:c + 1], None, A.mult)
+    tables(True)
 
     def blk(buf, c):
         return buf[:, 128 * c:128 * c + 128]
 
     def spread(src, name, bank):
-        MM([(T[bank][:, c::16], blk(T.U, c), src[:, 0:32], True, True, "U " + name) for c in range(16)], bank)
+        MM([(T[bank][:, c::16], blk(T.U, c), src[:], True, True, "U " + name) for c in range(16)], bank)
 
     dst = T.cores[(rank + SHIFT) % N]
     rid, pid, _ = topo.addr(dst)
     emask = topo.mask(core, dst)
     n_eng = len(topo.engines(core, dst))
+    Fwin, FWwin, Gwin = T.FB[:, 8:8 + W], T.FW[:, 0:W], T.G[:, 0:W]
+    XL, PL, OL, SL, zz = T.XL, T.PL, T.OL, T.SL, T.zz
+    xl = XL[:, 0:32]
 
     for k in range(STEPS):
         hN = "hb%d" % k
@@ -224,59 +303,52 @@ def rank_program(g, core, T, topo):
         MM([(T.pU[:, 0:32], blk(T.WS, c), h[:, c::16], c == 0, c == 15, "WS " + hN) for c in range(16)], "pU")
         V("cp", "pU", "ui", T.ui[:], T.pU[:, 0:32])
         V("ts", "ui", "um", T.um[:], T.ui[:], 4095, None, A.bitwise_and)
-        V("tt", "um", "sq", T.sq[:], T.um[:], T.um[:], A.mult)
-        V("ts", "sq", "sh", T.sh[:], T.sq[:], 5, None, A.arith_shift_right)
-        V("tt", "sh um", "z", T.z[:], T.sh[:], T.um[:], A.add)
-        V("ts", "z", "zz", T.zz[:], T.z[:], W - 16, None, A.bitwise_and)
-        V("ts", "zz pcol", "XL", T.XL[:], T.zz[:], pc, None, A.add)
-        Fwin, FWwin = T.FB[:, 8:8 + W], T.FW[:, 0:W]
-        V("tt", "FB XL DIAG", "gm", T.gm[:], Fwin.indirect(T.XL[:]), T.DIAG[:], A.mult)
-        ACT(T.Wn[:], FWwin.indirect(T.XL[:]), AF.Identity, "FW XL frac", "Wn", bias=T.frac[:, c1])
-        V("ts", "zz pcol", "XS", T.XS[:, 0::2], T.zz[:, 1::2], pc, None, A.add)
-        V("ts", "zz pcol", "XS", T.XS[:, 1::2], T.zz[:, 0::2], pc, None, A.add)
-        ACT(T.Ws[:], FWwin.indirect(T.XS[:]), AF.Identity, "FW XS frac", "Ws", bias=T.frac[:, c1])
-        ACT(T.ra[:], Fwin.indirect(T.XL[:]), AF.Copy, "FB XL", "ra")
-        MM([(T.pX[:], T.idn[:], h[:], True, False, "idn " + hN)], "pX")
+        V("ts", "um", "uo", T.uo[:], T.um[:], 32.0, None, A.add)
+        V("tt", "um uo", "sq", T.sq[:], T.um[:], T.uo[:], A.mult)
+        V("ts", "sq", "zz", zz[:], T.sq[:], 5, W - 16, A.arith_shift_right, A.bitwise_and)
+        V("ts", "zz pcol", "XL", XL[:, 0:32], zz[:], pc, None, A.add)
+        V("ts", "zz pcol", "XS", XL[:, 32::2], zz[:, 1::2], pc, None, A.add)
+        V("ts", "zz pcol", "XS", XL[:, 33::2], zz[:, 0::2], pc, None, A.add)
+        for a, ws in halves(16):
+            V("tt", "FB XL DIAG", "gm%d" % a, T.gm[:, 256 * a:256 * a + 256], Fwin.indirect(XL[:, ws]), T.DIAG[:], A.mult,
+              c=ga(256) / CYC)
+        for a in range(2):
+            ACT(T.Wg[:, 512 * a:512 * a + 512], FWwin.indirect(XL[:, 32 * a:32 * a + 32]), AF.Identity,
+                "FW fth " + ("XL", "XS")[a], "Wg%d" % a, ga(512) / CYC, bias=T.fth[:, c1])
+            V("tr", "Wg%d" % a, "WT", T.WT[:, 512 * a:512 * a + 512], T.Wg[:, 512 * a:512 * a + 512], c=512)
+        ACT(T.ra[:], Fwin.indirect(xl), AF.Copy, "FB XL", "ra", ga(512) / CYC)
+        V("tt", "zz kb", "key", T.key[:], zz[:], T.kb[:], A.add)
+        V("tt", "zz pmd", "xmd", T.xmd[:], zz[:], T.pmd[:], A.add)
+        it = []
+        for j in range(8):
+            it.append((T.pB[:, j:256:8], T.idn[:], T.key[:], True, j == 0, "idn key"))
+            if j:
+                it.append((T.pB[:, 9 * j:256:8], T.idm[:], T.key[:, 0:32 - j], False, True, "idm key"))
+        MM(it, "pB")
+        V("ts", "pB", "eq8", T.eq8[:], T.pB[:, 0:256], 0.0, None, A.is_equal, c=256)
 
         for hop in range(4):
             e, eN = (T.e0, "e0") if hop == 0 else (T.e, "e")
             ep, epN = (T.ep0, "ep0") if hop == 0 else (T.ep, "ep")
             thr, thN = (T.thr0, "thr0") if hop == 0 else (T.thr, "thr")
+            for a, ws in halves(16):
+                cs = slice(256 * a, 256 * a + 256)
+                if hop:
+                    V("tt", "WT OL DIAG", "gm%d" % a, T.gm[:, cs], T.WT[:, 0:W].indirect(OL[:, ws]), T.DIAG[:], A.mult,
+                      c=ga(256) / CYC)
+                V("scan", "RST gm%d" % a, "sc%d" % a, T.sc[:, cs], T.RST[:], T.gm[:, cs], 0.0, A.mult, A.add, c=256)
+                sc15 = T.sc[:, 256 * a + 15:256 * a + 256:16]
+                if hop == 0:
+                    V("cp", "sc%d" % a, "PL%d" % a, PL[:, ws], sc15)
+                else:
+                    V("ts", "sc%d" % a, "PL%d" % a, PL[:, ws], sc15, 1.0 / 4096.0, 4096.0 - HALF, A.mult, A.add)
+                V("tt", "hdrS PL%d %s" % (a, hN), "D%d" % a, T.D[:, cs], T.hdrS[:, 0:R].indirect(PL[:, ws]), h[:, cs],
+                  A.subtract, c=ga(256) / CYC)
+                ACT(T.Rn[:, cs], T.D[:, cs], AF.Abs, "D%d" % a, "Rn%d" % a, 256)
+            MM([(T.pD[:, 0:32], blk(T.S, c), T.Rn[:, c::16], c == 0, c == 15, "S Rn0 Rn1") for c in range(16)], "pD")
             if hop:
-                V("tt", "WT OL DIAG", "gm", T.gm[:], T.WT[:, 0:2 * P].indirect(T.OL[:]), T.DIAG[:], A.mult)
-            V("scan", "RST gm", "sc", T.sc[:], T.RST[:], T.gm[:], 0.0, A.mult, A.add)
-            if hop == 0:
-                V("ts", "sc", "PL", T.PL[:], T.sc[:, 15::16], -1.0, None, A.add)
-            else:
-                V("ts", "sc", "pint", T.pint[:], T.sc[:, 15::16], 4096.0 - HALF, None, A.add)
-                V("cp", "pint", "PL", T.PL[:], T.pint[:])
-            V("tt", "hdrS PL " + hN, "D", T.D[:], T.hdrS[:, 0:R].indirect(T.PL[:]), h[:], A.subtract)
-            V("ts", "D", "Rn", T.Rn[:], T.D[:], 0.0, -2.0, A.min, A.mult)
-            MM([(T.pD[:, 0:32], blk(T.S, c), T.D[:, c::16], c == 0, False, "S D") for c in range(16)]
-               + [(T.pD[:, 0:32], blk(T.S, c), T.Rn[:, c::16], False, c == 15, "S Rn") for c in range(16)], "pD")
-            if hop:
-                V("tt", "sc pint", "t1", T.t1[:], T.sc[:, 15::16], T.pint[:], A.subtract)
-            if hop == 0:
-                V("tr", "Wn", "WT", T.WT[:, 0:P], T.Wn[:])
-                V("tr", "Ws", "WT", T.WT[:, P:2 * P], T.Ws[:])
-            elif hop == 1:
-                V("cp", "FB", "FBw", T.FB[:, 7:8], T.FB[:, 7 + W:8 + W])
-                V("ts", "t1", "thr", T.thr[:], T.t1[:], 4096.0, 4096.0, A.add, A.mult)
-                V("tt", "FB FBw pM", "MF", T.MF[:], T.FB[:, 7:7 + W], T.pM[:], A.mult)
-            elif hop == 2:
-                V("ts", "zz pcol", "xf", T.xf[:], T.zz[:], pc, None, A.add)
-                V("ts", "t1", "thr", T.thr[:], T.t1[:], 4096.0, 4096.0, A.add, A.mult)
-                V("scan", "NM0 NM1 MF", "G", T.G[:], T.NM[:], T.MF[:], 0.0, A.mult, A.add)
-                V("tt", "xf kb", "key", T.key[:], T.xf[:], T.kb[:], A.add)
-                V("tt", "xf dump", "xmd", T.xmd[:], T.xf[:], T.dump[:], A.subtract)
-            else:
-                MM([(T.pX[:], T.idh[:], T.D[:], False, True, "idh D")], "pX")
-                MM([(T.pA[:], T.idn[:], T.D[:], True, False, "idn D"),
-                    (T.pA[:], T.idn[:], T.Rn[:], False, True, "idn Rn")], "pA")
-                V("tt", "G XL ra", "dr", T.dr[:], T.G[:, 0:W].indirect(T.XL[:]), T.ra[:], A.subtract)
-                V("ts", "t1", "thr", T.thr[:], T.t1[:], 4096.0, 4096.0, A.add, A.mult)
-                for j in range(1, 8):
-                    V("tt", "key", "eq8", T.eq8[:, 9 * j::8], T.key[:, j:32], T.key[:, 0:32 - j], A.is_equal)
+                V("ts", "PL0 PL1", "p4", T.p4[:], PL[:, 0:32], -4096.0, 4096.0, A.add, A.mult)
+                V("tt", "sc0 sc1 p4", "thr", T.thr[:], T.sc[:, 15::16], T.p4[:], A.subtract)
             V("cp", "pD", "qi", T.qi[:], T.pD[:, 0:32])
             V("tt", "pD " + thN, "ge", T.ge[:], T.pD[:, 0:32], thr[:], A.is_ge if hop < 3 else A.is_lt)
             V("ts", "qi", "q", T.q[:], T.qi[:], 2, 15, A.arith_shift_right, A.bitwise_and)
@@ -284,62 +356,53 @@ def rank_program(g, core, T, topo):
                 V("tt", "q " + eN, "dq", T.dq[:], T.q[:], e[:], A.subtract)
                 V("tt", "dq ge", "pr", T.pr[:], T.dq[:], T.ge[:], A.mult)
                 V("tt", "pr " + epN, "ep", T.ep[:], T.pr[:], ep[:], A.add)
+                V("cp", "ep", "OL", OL[:, 0:32], T.ep[:])
                 V("tt", "pr " + eN, "e", T.e[:], T.pr[:], e[:], A.add)
-                V("cp", "ep", "OL", T.OL[:], T.ep[:])
-                if hop == 2:
-                    spread(T.e, "e", "pE")
-                    ACT(T.ab[:], T.pE[:], AF.Abs, "pE ncol", "ab", bias=T.ncol[:, c1])
-                    ACT(T.pK[:], T.ab[:], AF.Relu, "ab", "pK", bias=1.0, scale=-1.0)
             else:
                 V("tt", "q e", "eqn", T.eqn[:], T.q[:], T.e[:], A.is_equal)
                 V("tt", "ge eqn", "done", T.done[:], T.ge[:], T.eqn[:], A.max)
+            if hop == 2:
+                spread(T.e, "e", "pE")
+                ACT(T.ab[:], T.pE[:], AF.Abs, "pE ncol", "ab", bias=T.ncol[:, c1])
+                ACT(T.pK[:], T.ab[:], AF.Relu, "ab", "pK", bias=1.0, scale=-1.0)
+                V("tt", "G XL ra", "dr", T.dr[:], Gwin.indirect(xl), T.ra[:], A.subtract, c=ga(512) / CYC)
+                V("tt", "dr pK", "tt", T.tt[:], T.dr[:], T.pK[:], A.mult, c=512)
 
         spread(T.done, "done", "pE")
+        MM([(T.pX[:], T.idn[:], h[:], True, False, "idn " + hN),
+            (T.pX[:], T.idh[:], T.D[:], False, True, "idh D0 D1")], "pX", 512)
+        ACT(T.y[:], T.pX[:], AF.Identity, "pX", "y", bias=BIG, scale=1.0 - 2.0 ** -11)
+        ACT(T.pB[:], T.y[:], AF.Copy, "y", "pB", bias=-BIG)
+        V("tt", "pB Rn0 Rn1", "Q", T.Q[:], T.pB[:], T.Rn[:], A.subtract, c=512)
+        hn, nx, arr, loc = "hn%d" % k, "hb%d" % (k + 1), "arr%d" % k, "loc%d" % k
+        for a, cs in halves(256):
+            V("tt", "Q pE pX", "t2_%d" % a, T.pX[:, cs], T.Q[:, cs], T.pE[:, cs], A.mult, c=256)
+        for a, cs in halves(256):
+            V("tt", "t2_%d pX Rn%d" % (a, a), hn, T[hn][:, cs], T.pX[:, cs], T.Rn[:, cs], A.add, c=256)
+        node("P", [((lambda hn=hn, nx=nx, arr=arr, loc=loc: g.remote_dma(
+            T[nx][:], T[hn][:], T.sem[arr], T.sem[loc], pid, rid, emask)), [hn])], [hn], [nx], SEND, FLY, (arr, 0))
+        nodes[-1]["remote"] = [(arr, n_eng), (loc, n_eng)]
         MM([(T.pU[:, 0:256], T.idn[:], T.eq8[:], True, False, "idn eq8")]
            + [(T.pU[:, 9 * j:256:8], T.idm[:], T.done[:, 0:32 - j], False, j == 7, "idm done")
               for j in range(1, 8)], "pU")
+        V("scan", "rst8 pU", "ls", T.ls[:], T.rst8[:], T.pU[:, 0:256], 0.0, A.mult, A.max, c=256)
         V("ts", "done", "win", T.win[:], T.done[:], 0.0, None, A.is_equal)
-        V("ts", "pX", "Bi", T.Bi[:], T.pX[:], -0.25, None, A.add)
-        V("tt", "Bi pA", "Q", T.Q[:], T.Bi[:], T.pA[:], A.subtract)
-        V("tt", "Q pE", "t2", T.t2[:], T.Q[:], T.pE[:], A.mult)
-        hn = "hn%d" % k
-        V("tt", "t2 pA", hn, T[hn][:], T.t2[:], T.pA[:], A.add)
-        wait_for("P", deps_of("P", [hn], []))
-        arr, loc, nxt = "arr%d" % k, "loc%d" % k, "hb%d" % (k + 1)
-        g.remote_dma(T[nxt][:], T[hn][:], T.sem[arr], T.sem[loc], pid, rid, emask)
-        for s in (arr, loc):
-            total[s] = n_eng
-            clock[(s, n_eng)] = {}
-        lastw[nxt] = (arr, n_eng)
-
-        V("scan", "rst8 pU", "ls", T.ls[:], T.rst8[:], T.pU[:, 0:256], 0.0, A.mult, A.max)
-        V("tt", "dr pK", "tt", T.tt[:], T.dr[:], T.pK[:], A.mult)
         V("tt", "win ls", "win", T.win[:], T.win[:], T.ls[:, 7::8], A.is_gt)
         V("tt", "win xmd", "m1", T.m1[:], T.win[:], T.xmd[:], A.mult)
         V("tt", "m1 dump", "off", T.off[:], T.m1[:], T.dump[:], A.add)
-        V("cp", "off", "SL", T.SL[:], T.off[:])
+        V("cp", "off", "SL", SL[:, 0:32], T.off[:])
         for j in reversed(range(4)):
             cs = slice(128 * j, 128 * j + 128)
-            V("tt", "SL tt ra L", "L", T.L[:, 0:W + 128].indirect(T.SL[:, 8 * j:8 * j + 8]),
-              T.tt[:, cs], T.ra[:, cs], A.add)
+            V("tt", "SL tt ra TB", "TB", T.TB[:, 0:W + 128].indirect(SL[:, 8 * j:8 * j + 8]),
+              T.tt[:, cs], T.ra[:, cs], A.add, c=(50 + 128 * 2.9) / CYC)
         if k < STEPS - 1:
-            for hf, cs in halves():
-                ACT(T.NM[:, cs], T.L[:, cs], AF.Relu, "L", "NM%d" % hf, bias=1.0, scale=-1.0)
-            fill_F()
-            for hf, cs in halves():
-                ACT(T.pM[:, cs], T.L[:, cs], AF.Sign, "L", "pM")
-            fill_FW()
+            tables(False)
 
     for hf, cs in halves():
-        bank, pm = ("pX", "pU") if hf == 0 else ("pA", "pD")
-        ACT(T[pm][:], T.L[:, cs], AF.Relu, "L", pm, bias=1.0, scale=-1.0)
-        ACT(T.Lm[:, cs], T.L[:, cs], AF.Copy, "L", "Lm%d" % hf, bias=-1.0)
-        V("tt", "ow1 " + pm, bank, T[bank][:], T.ow1[:, cs], T[pm][:], A.mult)
-        V("tt", ("Lm%d " % hf) + bank, "yoS%d" % hf, T.yoS[:, cs], T.Lm[:, cs], T[bank][:], A.add)
-    ACT(T.ymS[:], T.L[:, 0:W], AF.Sign, "L", "ymS")
-    for hf, cs in halves():
-        dma("A", T.yo[:, cs], T.yoS[:, cs], "st_yo%d" % hf, ["yoS%d" % hf], [])
-    dma("A", T.ym[:], T.ymS[0::16, :], "st_ym", ["ymS"], [])
-    dma("Y", T.yh[:], T["hb%d" % STEPS][:], "st_yh", ["hb%d" % STEPS], [])
-    for s, v in total.items():
-        g.wait_ge(T.sem[s], v)
+        ACT(T.AL[:, cs], T.TB[:, cs], AF.Abs, "TB", "AL%d" % hf, bias=4096.0)
+        V("ts", "AL%d" % hf, "yoS%d" % hf, T.yoS[:, cs], T.AL[:, cs], -4096.0, None, A.add, c=512)
+        dma(T.yo[:, cs], T.yoS[:, cs], "st_yo%d" % hf, ["yoS%d" % hf], [])
+    V("ts", "TB", "ymS", T.ymS[:], T.TB[:, 0:W], 0.0, None, A.is_ge, c=1024)
+    dma(T.ym[:], T.ymS[0::16, :], "st_ym", ["ymS"], [])
+    dma(T.yh[:], T["hb%d" % STEPS][:], "st_yh", ["hb%d" % STEPS], [])
+    issue(schedule())

from concourse.mybir import dt, AluOpType, AxisListType, ActivationFunctionType

N, W, R, P, STEPS, SHIFT = 6, 1024, 8192, 512, 3, 2
F32, BF, I32, U16 = "float32", "bfloat16", "int32", "uint16"
SCRATCH = {}


def sb(dtype, cols, names):
    for n in names.split():
        SCRATCH[n] = ("psum" if n[0] == "p" and n[1].isupper() else "sbuf", [128, cols], dtype)


sb(BF, R, "hdrS")
sb(I32, W, "owS mkS")
sb(F32, W, "o4 o5 FW G NM MF AL sg yoS ymS pM Wg WT")
sb(BF, W, "mkB")
sb(F32, W + 128, "TB")
sb(F32, W + 16, "FB")
sb(BF, 2048, "S WS U")
sb(BF, 128, "ones rep8 bones idn idh idm tmpa tmpc")
sb(BF, 16, "wS g8 g8w tmpb")
sb(I32, 8, "thS pi ci gi")
sb(F32, 8, "pcol ncol gcol coef thc fth")
sb(F32, 256, "jmod DIAG RST rst8 ls")
sb(F32, 32, "bpar b16 ne nb base ep0 dmp dump pmd kb one32 e0 thr0 xmd p4 thr ge dq pr ep eqn win m1 off")
sb(F32, P, "pU pD pE pK pX pB gm sc ra dr tt y")
sb(BF, P, "D Rn ab Q hb0 hb1 hb2 hb3 hn0 hn1 hn2")
sb(BF, 256, "eq8")
sb(I32, 32, "ui um uo sq zz qi q")
sb(BF, 32, "key e done")
sb(U16, 64, "XL PL OL SL")
LOADS = ["marks", "owner", "w", "th", "h0", "hdr"]
SEMAPHORES = ["V", "A", "T", "P"] + ["ld_" + n for n in LOADS] \
    + [n + str(k) for n in ("arr", "loc") for k in range(STEPS)] + ["st_yo0", "st_yo1", "st_ym", "st_yh"]
TH_TOP = 4081.0
HALF = 2041.0 / 4096.0
BIG = 8388608.0
CYC, PE, WAKE, DMA, SEND, FLY = 0.83, 0.6, 80, 2000, 1200, 2800
LOOK, TOL = 300, 60


def rank_program(g, core, T, topo):
    rank = T.rank_of(core)
    if rank is None:
        return
    A, AF = AluOpType, ActivationFunctionType
    queues = {"V": g.vector, "A": g.scalar, "T": g.tensor, "P": g, "Y": g.sync}
    nodes = []

    def node(q, emit, reads, writes, cost, lat=0.0, sem=None, early=0.0):
        nodes.append({"q": q, "emit": emit, "r": reads, "w": writes, "cost": cost, "lat": lat, "sem": sem or (q, 1),
                      "early": early})

    def op(q, fn, reads, writes, cost):
        node(q, [(fn, reads)], reads, writes, cost)

    vec = {"tt": g.vector.tensor_tensor, "ts": g.vector.tensor_scalar, "cp": g.vector.tensor_copy,
           "scan": g.vector.tensor_tensor_scan, "tr": g.vector.transpose, "ms": g.vector.memset}

    def V(name, reads, writes, *args, c=64):
        op("V", lambda: vec[name](*args), reads.split(), writes.split(), c * CYC)

    def ACT(out, in_, func, reads, writes, c=512, bias=0.0, scale=1.0):
        op("A", lambda: g.scalar.activation(out, in_, func, bias=bias, scale=scale), reads.split(), writes.split(),
           c * CYC)

    def MM(items, bank, n=64):
        emit = [((lambda it=it: g.tensor.matmul(it[0], it[1], it[2], it[3], it[4])), it[5].split()) for it in items]
        node("T", emit, [r for e in emit for r in e[1]], [bank], len(items) * n * PE)

    def dma(out, in_, sem, reads, writes, lat=DMA, early=0.0):
        node("Y", [((lambda: g.sync.dma_start(out, in_)), reads)], reads, writes, 60, lat, (sem, 16), early)

    def ga(n):
        return 60 + 1.5 * n

    def is_bank(r):
        return r[0] == "p" and r[1].isupper()

    def schedule():
        lastw, rd = {}, {}
        preds = []
        for i, d in enumerate(nodes):
            ps = set()
            for r in d["r"]:
                if r in lastw:
                    ps.add(lastw[r])
                if is_bank(r):
                    ps.update(rd.get(r, ()))
            for w in d["w"]:
                if w in lastw:
                    ps.add(lastw[w])
                ps.update(rd.get(w, ()))
            ps.discard(i)
            preds.append(ps)
            for r in d["r"]:
                rd.setdefault(r, []).append(i)
            for w in d["w"]:
                lastw[w] = i
                rd[w] = []
        n = len(nodes)
        succ = [[] for _ in range(n)]
        for i, ps in enumerate(preds):
            for p in ps:
                succ[p].append(i)
        prio = [0.0] * n
        for i in range(n - 1, -1, -1):
            d = nodes[i]
            prio[i] = d["cost"] + d["lat"] + max([prio[s] + WAKE for s in succ[i]] + [0.0])
        left = [len(p) for p in preds]
        avail = [0.0] * n
        ready = [i for i in range(n) if not left[i]]
        free = {q: 0.0 for q in queues}
        order = []
        while ready:
            st = {i: max(free[nodes[i]["q"]], avail[i]) for i in ready}
            t = min(st.values())
            q = nodes[min(ready, key=lambda i: (st[i], i))]["q"]
            cand = sorted([i for i in ready if nodes[i]["q"] == q and st[i] <= t + LOOK],
                          key=lambda j: (-prio[j] - nodes[j]["early"], j))
            i = cand[0]
            for j in cand:
                if st[j] <= t + 30 and t + nodes[j]["cost"] <= st[i] + TOL:
                    i = j
                    break
            d = nodes[i]
            ready.remove(i)
            order.append(i)
            free[q] = st[i] + d["cost"]
            for s in succ[i]:
                avail[s] = max(avail[s], free[q] + d["lat"] + WAKE)
                left[s] -= 1
                if not left[s]:
                    ready.append(s)
        return order

    def issue(order):
        known = {q: {} for q in queues}
        clock, total, lastw, rd = {}, {}, {}, {}

        def wait_for(q, deps):
            best = {}
            for s, v in deps:
                best[s] = max(v, best.get(s, 0))
            todo = [(s, v) for s, v in best.items() if known[q].get(s, 0) < v]
            todo = [d for d in todo if not any(o != d and clock[o].get(d[0], 0) >= d[1] for o in todo)]
            for s, v in todo:
                queues[q].wait_ge(T.sem[s], v)
                for a, b in clock[(s, v)].items():
                    known[q][a] = max(b, known[q].get(a, 0))
                known[q][s] = max(v, known[q].get(s, 0))

        for i in order:
            d = nodes[i]
            q, (sem, inc) = d["q"], d["sem"]
            ins = None
            for j, (fn, reads) in enumerate(d["emit"]):
                deps = []
                for r in reads:
                    if r in lastw:
                        deps.append(lastw[r])
                    if is_bank(r):
                        deps += [x for x in rd.get(r, {}).items() if x[0] != sem]
                for w in d["w"] if j == 0 else []:
                    if w in lastw and lastw[w][0] != sem:
                        deps.append(lastw[w])
                    deps += [x for x in rd.get(w, {}).items() if x[0] != sem]
                wait_for(q, deps)
                ins = fn()
            if inc == 0:
                key, rkey = d["remote"]
                for s, v in (key, rkey):
                    total[s] = v
                    clock[(s, v)] = {}
            else:
                ins.then_inc(T.sem[sem], inc)
                total[sem] = total.get(sem, 0) + inc
                clock[(sem, total[sem])] = dict(known[q])
                key = rkey = (sem, total[sem])
            for r in d["r"]:
                rd.setdefault(r, {})[rkey[0]] = rkey[1]
            for w in d["w"]:
                lastw[w] = key
                rd[w] = {}
        for s, v in total.items():
            g.wait_ge(T.sem[s], v)

    def halves(n=512):
        return [(hf, slice(hf * n, hf * n + n)) for hf in range(2)]

    c1 = slice(0, 1)
    dma(T.mkS[0:8, :], T.marks[:], "ld_marks", [], ["mkS"], early=9e6)
    dma(T.owS[:], T.owner[:], "ld_owner", [], ["owS"], 4000, early=8e6)
    dma(T.wS[:, c1], T.w[:], "ld_w", [], ["wS"], 5000, early=7e6)
    dma(T.thS[:, c1], T.th[:], "ld_th", [], ["thS"], 5000, early=6e6)
    dma(T.hb0[:], T.h0[:], "ld_h0", [], ["hb0"], 5500, early=5e6)
    dma(T.hdrS[:], T.hdr[:], "ld_hdr", [], ["hdrS"], 12000)

    def iota(buf, name, pattern, base, cm, c):
        op("P", lambda: g.iota(buf, pattern, base, cm, allow_small_or_imprecise_dtypes=True), [], [name], 150 + 2 * c)

    def sel(out, in_, pattern, cmp, base, cm, reads, writes, c):
        op("P", lambda: g.affine_select(out, in_, pattern, cmp, 0.0, base, cm), [reads], [writes], 170 + 2 * c)

    V("ms", "", "ones", T.ones[:], 1.0)
    op("P", lambda: g.iota(T.pi[:, c1], [[0, 1]], 0, 1), [], ["pi"], 150)
    sel(T.tmpc[0:8, :], T.ones[0:8, :], [[1, 128]], A.is_ge, 0, -16, "ones", "tmpc", 128)
    sel(T.rep8[0:8, :], T.tmpc[0:8, :], [[-1, 128]], A.is_ge, 15, 16, "tmpc", "rep8", 128)
    V("cp", "mkS", "mkB", T.mkB[0:8, :], T.mkS[0:8, :], c=1024)
    for hf, cs in halves():
        MM([(T.pM[:, cs], T.rep8[0:8, :], T.mkB[0:8, cs], True, True, "rep8 mkB")], "pM", 512)
    for hf, cs in halves():
        sg = ("pE", "pK")[hf]
        ACT(T[sg][:], T.pM[:, cs], AF.Copy, "pM", sg, bias=-1.0, scale=2.0)
        V("ts", "owS", "o4_%d" % hf, T.o4[:, cs], T.owS[:, cs], 4096.0, None, A.add, c=512)
        V("tt", "o4_%d %s" % (hf, sg), "o5_%d" % hf, T.o5[:, cs], T.o4[:, cs], T[sg][:], A.mult, c=512)
        ACT(T.TB[:, cs], T.o5[:, cs], AF.Copy, "o5_%d" % hf, "TB", bias=-4096.0)

    def tables(first):
        for hf, cs in halves():
            ACT(T.AL[:, cs], T.TB[:, cs], AF.Abs, "TB", "AL%d" % hf)
        for hf, cs in halves():
            fs = slice(8 + 512 * hf, 520 + 512 * hf)
            V("scan", ("AL%d TB" % hf) + (" FB" if hf else ""), "FB", T.FB[:, fs],
              T.AL[:, cs], T.TB[:, cs], T.FB[:, 519:520] if hf else 0.0, A.min, A.max, c=512)
        for hf, cs in halves():
            fs = slice(8 + 512 * hf, 520 + 512 * hf)
            ACT(T.FW[:, cs], T.FB[:, fs], AF.Copy, "FB", "FW", bias=-16777216.0, scale=4096.0)
        if first:
            ACT(T.NM[:], T.pM[:], AF.Copy, "pM", "NM", 1024, bias=1.0, scale=-1.0)
        else:
            ACT(T.sg[:], T.TB[:, 0:W], AF.Sign, "TB", "sg", 1024, bias=0.5)
            ACT(T.pM[:], T.sg[:], AF.Relu, "sg", "pM", 1024)
            ACT(T.NM[:], T.sg[:], AF.Relu, "sg", "NM", 1024, scale=-1.0)
        V("cp", "FB", "FBw", T.FB[:, 7:8], T.FB[:, 7 + W:8 + W])
        V("tt", "FB FBw pM", "MF0", T.MF[:, 0:512], T.FB[:, 7:519], T.pM[:, 0:512], A.mult, c=512)
        V("tt", "FB pM", "MF1", T.MF[:, 512:], T.FB[:, 519:7 + W], T.pM[:, 512:], A.mult, c=512)
        V("scan", "NM MF0", "G", T.G[:, 0:512], T.NM[:, 0:512], T.MF[:, 0:512], 0.0, A.mult, A.add, c=512)
        V("scan", "NM MF1 G", "G", T.G[:, 512:], T.NM[:, 512:], T.MF[:, 512:], T.G[:, 511:512], A.mult, A.add, c=512)

    sel(T.tmpb[:, 0:8], T.ones[:, 0:8], [[-16, 8]], A.is_ge, 0, 1, "ones", "tmpb", 8)
    sel(T.g8[:, 0:8], T.tmpb[:, 0:8], [[16, 8]], A.is_ge, 15, -1, "tmpb", "g8", 8)
    iota(T.jmod[:], "jmod", [[0, 16], [1, 16]], 0, 0, 256)
    sel(T.tmpa[:], T.ones[:], [[-16, 8], [0, 16]], A.is_ge, 0, 1, "ones", "tmpa", 128)
    sel(T.bones[:], T.tmpa[:], [[16, 8], [0, 16]], A.is_ge, 15, -1, "tmpa", "bones", 128)
    sel(T.idn[:], T.ones[:], [[-1, 128]], A.is_equal, 0, 1, "ones", "idn", 128)
    iota(T.bpar[:], "bpar", [[0, 16], [1, 2]], 0, 0, 32)
    iota(T.b16[:], "b16", [[16, 32]], 0, 0, 32)
    iota(T.dmp[:], "dmp", [[0, 4], [16, 8]], W, 0, 32)
    iota(T.kb[:], "kb", [[0, 2], [W, 2], [0, 8]], W, 0, 32)
    iota(T.rst8[:], "rst8i", [[0, 32], [1, 8]], 0, 0, 256)
    V("ms", "", "S", T.S[:], 0.0, c=1024)
    V("ms", "", "WS", T.WS[:], 0.0, c=1024)
    V("ms", "", "one32", T.one32[:], 1.0)
    V("ts", "pi", "ci", T.ci[:, c1], T.pi[:, c1], 15, None, A.bitwise_and)
    V("ts", "pi", "gi", T.gi[:, c1], T.pi[:, c1], 4, 1, A.arith_shift_right, A.bitwise_and)
    V("cp", "ci", "pcol", T.pcol[:, c1], T.ci[:, c1])
    V("cp", "gi", "gcol", T.gcol[:, c1], T.gi[:, c1])
    V("ts", "pcol", "ncol", T.ncol[:, c1], T.pcol[:, c1], -1.0, None, A.mult)
    V("ts", "gcol", "coef", T.coef[:, c1], T.gcol[:, c1], 32.0, 496.0, A.mult, A.add)
    V("cp", "thS", "thc", T.thc[:, c1], T.thS[:, c1])
    V("ts", "thc", "fth", T.fth[:, c1], T.thc[:, c1], TH_TOP, None, A.min)
    V("ts", "g8 wS", "g8w", T.g8w[:, 0:8], T.g8[:, 0:8], T.wS[:, c1], None, A.mult)
    for c in range(16):
        V("cp", "g8w", "WS", T.WS[:, 129 * c:128 * (c + 1):16], T.g8w[:, 0:8])
    for c in range(16):
        ACT(T.S[:, 129 * c:128 * (c + 1):16], T.g8[:, 0:8], AF.Copy, "g8", "S", 64)
    pc = T.pcol[:, c1]
    V("ts", "jmod pcol", "DIAG", T.DIAG[:], T.jmod[:], pc, None, A.is_equal, c=256)
    V("ts", "jmod", "RST", T.RST[:], T.jmod[:], 0.0, None, A.not_equal, c=256)
    V("ts", "bpar gcol", "ne", T.ne[:], T.bpar[:], T.gcol[:, c1], None, A.not_equal)
    V("ts", "ne coef", "nb", T.nb[:], T.ne[:], T.coef[:, c1], None, A.mult)
    V("tt", "nb b16", "base", T.base[:], T.nb[:], T.b16[:], A.add)
    V("ts", "base pcol", "ep0", T.ep0[:], T.base[:], pc, None, A.add)
    V("ts", "one32 pcol", "e0", T.e0[:], T.one32[:], pc, None, A.mult)
    V("ts", "one32 thc", "thr0", T.thr0[:], T.one32[:], T.thc[:, c1], None, A.mult)
    V("ts", "dmp pcol", "dump", T.dump[:], T.dmp[:], pc, None, A.add)
    V("ts", "dmp", "pmd", T.pmd[:], T.dmp[:], -1.0, None, A.mult)
    V("ts", "idn", "idh", T.idh[:], T.idn[:], 0.5, None, A.mult)
    V("ts", "idn", "idm", T.idm[:], T.idn[:], -1.0, None, A.mult)
    V("ts", "rst8i", "rst8", T.rst8[:], T.rst8[:], 0.0, None, A.not_equal, c=256)
    for c in range(16):
        V("ts", "bones DIAG", "U", T.U[:, 128 * c:128 * c + 128], T.bones[:], T.DIAG[:, c:c + 1], None, A.mult)
    tables(True)

    def blk(buf, c):
        return buf[:, 128 * c:128 * c + 128]

    def spread(src, name, bank):
        MM([(T[bank][:, c::16], blk(T.U, c), src[:], True, True, "U " + name) for c in range(16)], bank)

    dst = T.cores[(rank + SHIFT) % N]
    rid, pid, _ = topo.addr(dst)
    emask = topo.mask(core, dst)
    n_eng = len(topo.engines(core, dst))
    Fwin, FWwin, Gwin = T.FB[:, 8:8 + W], T.FW[:, 0:W], T.G[:, 0:W]
    XL, PL, OL, SL, zz = T.XL, T.PL, T.OL, T.SL, T.zz
    xl = XL[:, 0:32]

    for k in range(STEPS):
        hN = "hb%d" % k
        h = T[hN]
        MM([(T.pU[:, 0:32], blk(T.WS, c), h[:, c::16], c == 0, c == 15, "WS " + hN) for c in range(16)], "pU")
        V("cp", "pU", "ui", T.ui[:], T.pU[:, 0:32])
        V("ts", "ui", "um", T.um[:], T.ui[:], 4095, None, A.bitwise_and)
        V("ts", "um", "uo", T.uo[:], T.um[:], 32.0, None, A.add)
        V("tt", "um uo", "sq", T.sq[:], T.um[:], T.uo[:], A.mult)
        V("ts", "sq", "zz", zz[:], T.sq[:], 5, W - 16, A.arith_shift_right, A.bitwise_and)
        V("ts", "zz pcol", "XL", XL[:, 0:32], zz[:], pc, None, A.add)
        V("ts", "zz pcol", "XS", XL[:, 32::2], zz[:, 1::2], pc, None, A.add)
        V("ts", "zz pcol", "XS", XL[:, 33::2], zz[:, 0::2], pc, None, A.add)
        for a, ws in halves(16):
            V("tt", "FB XL DIAG", "gm%d" % a, T.gm[:, 256 * a:256 * a + 256], Fwin.indirect(XL[:, ws]), T.DIAG[:], A.mult,
              c=ga(256) / CYC)
        for a in range(2):
            ACT(T.Wg[:, 512 * a:512 * a + 512], FWwin.indirect(XL[:, 32 * a:32 * a + 32]), AF.Identity,
                "FW fth " + ("XL", "XS")[a], "Wg%d" % a, ga(512) / CYC, bias=T.fth[:, c1])
            V("tr", "Wg%d" % a, "WT", T.WT[:, 512 * a:512 * a + 512], T.Wg[:, 512 * a:512 * a + 512], c=512)
        ACT(T.ra[:], Fwin.indirect(xl), AF.Copy, "FB XL", "ra", ga(512) / CYC)
        V("tt", "zz kb", "key", T.key[:], zz[:], T.kb[:], A.add)
        V("tt", "zz pmd", "xmd", T.xmd[:], zz[:], T.pmd[:], A.add)
        it = []
        for j in range(8):
            it.append((T.pB[:, j:256:8], T.idn[:], T.key[:], True, j == 0, "idn key"))
            if j:
                it.append((T.pB[:, 9 * j:256:8], T.idm[:], T.key[:, 0:32 - j], False, True, "idm key"))
        MM(it, "pB")
        V("ts", "pB", "eq8", T.eq8[:], T.pB[:, 0:256], 0.0, None, A.is_equal, c=256)

        for hop in range(4):
            e, eN = (T.e0, "e0") if hop == 0 else (T.e, "e")
            ep, epN = (T.ep0, "ep0") if hop == 0 else (T.ep, "ep")
            thr, thN = (T.thr0, "thr0") if hop == 0 else (T.thr, "thr")
            for a, ws in halves(16):
                cs = slice(256 * a, 256 * a + 256)
                if hop:
                    V("tt", "WT OL DIAG", "gm%d" % a, T.gm[:, cs], T.WT[:, 0:W].indirect(OL[:, ws]), T.DIAG[:], A.mult,
                      c=ga(256) / CYC)
                V("scan", "RST gm%d" % a, "sc%d" % a, T.sc[:, cs], T.RST[:], T.gm[:, cs], 0.0, A.mult, A.add, c=256)
                sc15 = T.sc[:, 256 * a + 15:256 * a + 256:16]
                if hop == 0:
                    V("cp", "sc%d" % a, "PL%d" % a, PL[:, ws], sc15)
                else:
                    V("ts", "sc%d" % a, "PL%d" % a, PL[:, ws], sc15, 1.0 / 4096.0, 4096.0 - HALF, A.mult, A.add)
                V("tt", "hdrS PL%d %s" % (a, hN), "D%d" % a, T.D[:, cs], T.hdrS[:, 0:R].indirect(PL[:, ws]), h[:, cs],
                  A.subtract, c=ga(256) / CYC)
                ACT(T.Rn[:, cs], T.D[:, cs], AF.Abs, "D%d" % a, "Rn%d" % a, 256)
            MM([(T.pD[:, 0:32], blk(T.S, c), T.Rn[:, c::16], c == 0, c == 15, "S Rn0 Rn1") for c in range(16)], "pD")
            if hop:
                V("ts", "PL0 PL1", "p4", T.p4[:], PL[:, 0:32], -4096.0, 4096.0, A.add, A.mult)
                V("tt", "sc0 sc1 p4", "thr", T.thr[:], T.sc[:, 15::16], T.p4[:], A.subtract)
            V("cp", "pD", "qi", T.qi[:], T.pD[:, 0:32])
            V("tt", "pD " + thN, "ge", T.ge[:], T.pD[:, 0:32], thr[:], A.is_ge if hop < 3 else A.is_lt)
            V("ts", "qi", "q", T.q[:], T.qi[:], 2, 15, A.arith_shift_right, A.bitwise_and)
            if hop < 3:
                V("tt", "q " + eN, "dq", T.dq[:], T.q[:], e[:], A.subtract)
                V("tt", "dq ge", "pr", T.pr[:], T.dq[:], T.ge[:], A.mult)
                V("tt", "pr " + epN, "ep", T.ep[:], T.pr[:], ep[:], A.add)
                V("cp", "ep", "OL", OL[:, 0:32], T.ep[:])
                V("tt", "pr " + eN, "e", T.e[:], T.pr[:], e[:], A.add)
            else:
                V("tt", "q e", "eqn", T.eqn[:], T.q[:], T.e[:], A.is_equal)
                V("tt", "ge eqn", "done", T.done[:], T.ge[:], T.eqn[:], A.max)
            if hop == 2:
                spread(T.e, "e", "pE")
                ACT(T.ab[:], T.pE[:], AF.Abs, "pE ncol", "ab", bias=T.ncol[:, c1])
                ACT(T.pK[:], T.ab[:], AF.Relu, "ab", "pK", bias=1.0, scale=-1.0)
                V("tt", "G XL ra", "dr", T.dr[:], Gwin.indirect(xl), T.ra[:], A.subtract, c=ga(512) / CYC)
                V("tt", "dr pK", "tt", T.tt[:], T.dr[:], T.pK[:], A.mult, c=512)

        spread(T.done, "done", "pE")
        MM([(T.pX[:], T.idn[:], h[:], True, False, "idn " + hN),
            (T.pX[:], T.idh[:], T.D[:], False, True, "idh D0 D1")], "pX", 512)
        ACT(T.y[:], T.pX[:], AF.Identity, "pX", "y", bias=BIG, scale=1.0 - 2.0 ** -11)
        ACT(T.pB[:], T.y[:], AF.Copy, "y", "pB", bias=-BIG)
        V("tt", "pB Rn0 Rn1", "Q", T.Q[:], T.pB[:], T.Rn[:], A.subtract, c=512)
        hn, nx, arr, loc = "hn%d" % k, "hb%d" % (k + 1), "arr%d" % k, "loc%d" % k
        for a, cs in halves(256):
            V("tt", "Q pE pX", "t2_%d" % a, T.pX[:, cs], T.Q[:, cs], T.pE[:, cs], A.mult, c=256)
        for a, cs in halves(256):
            V("tt", "t2_%d pX Rn%d" % (a, a), hn, T[hn][:, cs], T.pX[:, cs], T.Rn[:, cs], A.add, c=256)
        node("P", [((lambda hn=hn, nx=nx, arr=arr, loc=loc: g.remote_dma(
            T[nx][:], T[hn][:], T.sem[arr], T.sem[loc], pid, rid, emask)), [hn])], [hn], [nx], SEND, FLY, (arr, 0))
        nodes[-1]["remote"] = [(arr, n_eng), (loc, n_eng)]
        MM([(T.pU[:, 0:256], T.idn[:], T.eq8[:], True, False, "idn eq8")]
           + [(T.pU[:, 9 * j:256:8], T.idm[:], T.done[:, 0:32 - j], False, j == 7, "idm done")
              for j in range(1, 8)], "pU")
        V("scan", "rst8 pU", "ls", T.ls[:], T.rst8[:], T.pU[:, 0:256], 0.0, A.mult, A.max, c=256)
        V("ts", "done", "win", T.win[:], T.done[:], 0.0, None, A.is_equal)
        V("tt", "win ls", "win", T.win[:], T.win[:], T.ls[:, 7::8], A.is_gt)
        V("tt", "win xmd", "m1", T.m1[:], T.win[:], T.xmd[:], A.mult)
        V("tt", "m1 dump", "off", T.off[:], T.m1[:], T.dump[:], A.add)
        V("cp", "off", "SL", SL[:, 0:32], T.off[:])
        for j in reversed(range(4)):
            cs = slice(128 * j, 128 * j + 128)
            V("tt", "SL tt ra TB", "TB", T.TB[:, 0:W + 128].indirect(SL[:, 8 * j:8 * j + 8]),
              T.tt[:, cs], T.ra[:, cs], A.add, c=(50 + 128 * 2.9) / CYC)
        if k < STEPS - 1:
            tables(False)

    for hf, cs in halves():
        ACT(T.AL[:, cs], T.TB[:, cs], AF.Abs, "TB", "AL%d" % hf, bias=4096.0)
        V("ts", "AL%d" % hf, "yoS%d" % hf, T.yoS[:, cs], T.AL[:, cs], -4096.0, None, A.add, c=512)
        dma(T.yo[:, cs], T.yoS[:, cs], "st_yo%d" % hf, ["yoS%d" % hf], [])
    V("ts", "TB", "ymS", T.ymS[:], T.TB[:, 0:W], 0.0, None, A.is_ge, c=1024)
    dma(T.ym[:], T.ymS[0::16, :], "st_ym", ["ymS"], [])
    dma(T.yh[:], T["hb%d" % STEPS][:], "st_yh", ["hb%d" % STEPS], [])
    issue(schedule())
